import numpy as np, ml_dtypes
CORES = [48,51,52,55]
N = 4
BF = ml_dtypes.bfloat16
def f(rng, *shape):
    return (rng.standard_normal(shape, dtype=np.float32) * np.exp2(rng.integers(-2, 3, shape[:-1] + (1,)))).astype(BF)
def wide(rng, *shape):
    v = f(rng, *shape).astype(np.float32); k = shape[:-2] + (1, shape[-1])
    return (v * np.exp2(rng.integers(-6, 7, k)) * (rng.random(k) > 0.0625)).astype(BF)
P, F, M, C, T, K, D = 4096, 512, 11, 2048, 4, 64, 5
def parts(rng):
    pic = rng.standard_normal((N, 8, 1, P), dtype=np.float32) + rng.standard_normal((N, 8, 16, P), dtype=np.float32)
    pic = (pic * np.exp2(rng.integers(-2, 3, (N, 8, 16, 1)))).astype(np.float32)
    s = rng.integers(0, P, (N, 8, 16, F)); o = rng.integers(0, P, (N, 8, 16, T)); th = M // 2 + rng.integers(-1, 2, (N, 8, T))
    return pic, s, o, th, rng.integers(-256, 257, (N, 8, 16, C)), rng.integers(0, P, (N, 8, 16, C))
def pack(pic, s, o, th, b, e):
    return {"pic": pic.reshape(N, 128, P).astype(BF), "shp": s.reshape(N, 128, F).astype(np.int32), "ofs": o.reshape(N, 128, T).astype(np.int32),
            "thr": th.astype(np.int32), "inc": b.reshape(N, 128, C).astype(np.float32).astype(BF), "ex": e.reshape(N, 128, C).astype(np.int32)}
def setup_inputs(rng):
    return pack(*parts(rng))
def setup_inputs_edge(rng):
    pic, s, o, th, b, e = parts(rng)
    lv = np.array([0, 3, 4, 8, 9, 11, 12, 16])[rng.integers(0, 8, (N, 8, 1, P))]; ch = np.argsort(rng.random((N, 8, 16, 1)), axis=2)
    pic = (ch < lv).astype(np.float32) * np.exp2(rng.integers(-2, 3, (N, 8, 16, 1)))
    return pack(pic, s, o, 3 * M // 4 + rng.integers(-1, 2, (N, 8, T)), b, e)
def setup_inputs_ends(rng):
    pic, s, o, th, b, e = parts(rng)
    s = rng.choice(np.array([0, 1, P // 2, P - 1]), s.shape); o = rng.choice(np.array([0, 1, P - 1]), o.shape)
    b = rng.choice(np.array([-256, -255, -2, -1, 0, 1, 255, 256]), b.shape); e[:, ::2] = rng.choice(np.array([0, 1, P - 1]), (N, 4, 16, C))
    th[:, :3] = 0; th[:, 3] = 16
    pic[:, 4] = -(np.arange(P) >> 5)
    x = np.arange(16)[:, None] * (P >> 4) + rng.integers(0, P >> 5, (N, 16, F))
    s[:, 4] = np.where(rng.random((N, 1, F)) < 0.5, P - 1 - x, x); o[:, 4, :, 0] = 0; th[:, 4, 0] = M
    return pack(pic, s, o, th, b, e)
def setup_inputs_mixed(rng):
    pic, s, o, th, b, e = parts(rng)
    x = np.arange(P); ch = np.argsort(rng.random((N, 3, 16, 1)), axis=2) < 10
    pic[:, :3] = np.where(ch | ((x & 1) == 0), -(x >> 5), x >> 5) * np.exp2(rng.integers(-2, 3, (N, 3, 16, 1)))
    code = rng.integers(0, C - 1, (N, 3, F)); odd = rng.integers(0, 2, (N, 3, F))
    code[:, 0, :K] = np.argsort(rng.random((N, C)), axis=1)[:, :K]; odd[:, 0, :K] = 0
    code[:, 1:, ::3] = C - 1; odd[:, 1, 0] = 0; odd[:, 1, 3] = 1; odd[:, 2, ::3] = 1; odd[:, 2, 1] = 0
    lv = np.zeros((N, 3, 16, F), np.int64)
    for m in range(M):
        lv[:, :, m + D] = lv[:, :, m] + 2 * ((code >> m) & 1) - 1
    at = (8 + lv) * (P >> 4) + rng.integers(0, P >> 5, lv.shape); at = at - (at & 1) + odd[:, :, None, :]
    s[:, :3] = (at - o[:, :3, :, :1]) & (P - 1)
    pic[:, 3] = rng.standard_normal((N, 16, P), dtype=np.float32)
    pic[:, 4:6] = 3 * rng.standard_normal((N, 2, 1, P), dtype=np.float32) + rng.standard_normal((N, 2, 16, P), dtype=np.float32)
    for g, w in enumerate(([M, 16, 0, 1], [1, 0, 0, 0], [1, 16, 0, M], [1, 1, 0, 1], [M, M - 1, 16, 0], [M - 1, 0, M, 16], [M // 2, 16, 0, M // 2], [13, 0, 14, 15])):
        th[:, g] = np.resize(np.array(w), T)
    return pack(pic, s, o, th, b, e)
def setup_inputs_repeat(rng):
    pic, s, o, th, b, e = parts(rng)
    s[:, ::2] = s[:, ::2][..., rng.integers(0, 5, F)]; th[:, ::2] = 0
    s[:, 6, :, :T * K] = rng.integers(0, P, (N, 16, T * K))
    pic[:, 2:4] = 1.0; th[:, 2] = M; th[:, 3] = M + 1
    return pack(pic, s, o, th, b, e)
def setup_inputs_spread(rng):
    pic, s, o, th, b, e = parts(rng); lp = P.bit_length() - 1
    w = wide(rng, N, 128, P).astype(np.float32).reshape(N, 8, 16, P)
    pic = np.where(rng.random((N, 8, 1, P)) < 0.5, np.abs(w), w) * np.exp2(rng.integers(-60, 61, (N, 8, 16, 1)))
    pic = np.where(np.abs(pic) < 2.0 ** -78, 0.0, pic)
    s = np.minimum(np.exp2(lp * rng.random(s.shape)).astype(np.int64), P - 1); e = np.minimum(np.exp2(lp * rng.random(e.shape)).astype(np.int64), P - 1)
    b = np.minimum(np.exp2(8 * rng.random(b.shape)).astype(np.int64), 256) * rng.integers(-1, 2, b.shape)
    return pack(pic, s, o, rng.integers(2, M - 1, (N, 8, T)), b, e)
def check_inputs(d):
    bad = []
    for k, lo, hi in (("shp", 0, P - 1), ("ofs", 0, P - 1), ("thr", 0, 16), ("ex", 0, P - 1)):
        if np.min(d[k]) < lo or np.max(d[k]) > hi: bad.append("range of " + k)
    p = np.abs(np.asarray(d["pic"]).astype(np.float32))
    if not np.all((p == 0) | ((p >= 2.0 ** -100) & (p <= 2.0 ** 100))): bad.append("sizes of pic")
    a = np.asarray(d["inc"]).astype(np.float32)
    if not (np.all(np.abs(a) <= 256) and np.all(a == np.floor(a))): bad.append("whole numbers of inc")
    return bad
def reference(pic, shp, ofs, thr, inc, ex):
    im = pic.astype(np.float32).reshape(N, 8, 16, P); s = shp.astype(np.int64).reshape(N, 8, 16, F); o = ofs.astype(np.int64).reshape(N, 8, 16, T)
    b = inc.astype(np.float32).astype(np.int64).reshape(N, 8, 16, C); e = ex.astype(np.int64).reshape(N, 8, 16, C); bit = 2 ** np.arange(M)[:, None]
    for t in range(T):
        d = D - t; after = np.array(b); new = []
        for r in range(N):
            q = (r + 1 + t) % N
            x = (s[r] + o[r, :, :, t:t + 1]) & (P - 1)
            v = np.take_along_axis(im[r], x.reshape(8, 1, 16 * F), 2).reshape(8, 16, 16, F)
            n = np.add.reduce((v[:, :, :M] > v[:, :, d:d + M]).astype(np.int64), axis=1)
            code = np.add.reduce((n >= 9) * bit, axis=1)
            sure = np.add.reduce(((n >= 12) | (n <= 3)).astype(np.int64), axis=1) >= thr[r][:, t:t + 1]
            up = np.take_along_axis(b[q], code[:, None, :], 2); like = np.take_along_axis(e[q], code[:, None, :], 2)
            new.append(np.where(sure[:, None, :], (s[r] + up) & (P - 1), like))
            used = np.zeros((8, C + 1), bool)
            np.put_along_axis(used, np.where(sure, code, C)[:, t * K:t * K + K], True, 1)
            after[q] = np.where(used[:, None, :C], b[q] >> 1, b[q])
        s = np.stack(new); b = after
    return {"ys": s.reshape(N, 128, F).astype(np.float32), "yi": b.reshape(N, 128, C).astype(np.float32).astype(BF)}

@@ -1,0 +1,358 @@
+from concourse.mybir import AluOpType, ActivationFunctionType
+
+N, P, F, M, C, NT, K = 4, 4096, 512, 11, 2048, 4, 64
+H = F // 2
+LO = 768
+PW = LO + 2 * P + LO
+Z0 = C + F
+SL = K + C
+TINY = 2.0 ** -108
+BF, F32, I32, U16 = "bfloat16", "float32", "int32", "uint16"
+
+SCRATCH = {
+    "pw": ("sbuf", [128, PW], BF), "u": ("sbuf", [128, F * 16], BF), "cmp": ("sbuf", [128, F, M], BF),
+    "w1": ("sbuf", [128, Z0 + 5 * SL], BF),
+    "w20": ("sbuf", [128, C + F], I32), "w21": ("sbuf", [128, C + F], I32),
+    "w22": ("sbuf", [128, C + F], I32), "w23": ("sbuf", [128, C + F], I32),
+    "xi": ("sbuf", [128, F], I32), "xj": ("sbuf", [128, F], I32), "yf": ("sbuf", [128, F], F32), "off": ("sbuf", [128, F], U16),
+    "up": ("sbuf", [128, F], BF),
+    "ft0": ("sbuf", [128, 48, M], BF), "ft1": ("sbuf", [128, 48, M], BF), "one": ("sbuf", [128, 16, M], BF),
+    "ub": ("sbuf", [128, 32], F32), "tb": ("sbuf", [128, 64], F32), "il": ("sbuf", [128, 64], U16),
+    "ofi": ("sbuf", [128, 4], I32), "off32": ("sbuf", [128, 4], F32),
+    "thi": ("sbuf", [128, 4], I32), "thb": ("sbuf", [128, 8], BF), "thf": ("sbuf", [128, 4], F32),
+    "row": ("sbuf", [128, 144], F32), "big": ("sbuf", [128, SL], F32), "cst": ("sbuf", [128, 8], F32),
+    "pi": ("sbuf", [128, 4], I32), "pj": ("sbuf", [128, 4], I32), "pf": ("sbuf", [128, 4], F32),
+    "gi": ("sbuf", [128, 128], F32), "gm": ("sbuf", [128, 128], BF),
+    "ee": ("sbuf", [128, 144], BF), "eh": ("sbuf", [128, 144], BF), "idm": ("sbuf", [128, (M + 1) * 128], BF),
+    "fi": ("sbuf", [128, 48], F32), "ff": ("sbuf", [128, 48], F32),
+    "ki": ("sbuf", [128, 256], F32), "kc": ("sbuf", [128, 256], BF),
+    "y0": ("sbuf", [128, 4], F32), "yl": ("sbuf", [128, 4], U16), "ne": ("sbuf", [128, 256], BF),
+    "kp": ("sbuf", [128, 256], BF), "ym": ("sbuf", [128, 4], F32), "tl": ("sbuf", [128, 4], U16),
+    "mo0": ("sbuf", [128, 68], I32), "mo1": ("sbuf", [128, 68], I32), "mo2": ("sbuf", [128, 68], I32), "mo3": ("sbuf", [128, 68], I32),
+    "mi1": ("sbuf", [128, 68], I32), "mi2": ("sbuf", [128, 68], I32), "mi3": ("sbuf", [128, 68], I32),
+    "cp0": ("psum", [128, 128, 8], F32), "cp1": ("psum", [128, 128, 8], F32),
+    "vp0": ("psum", [128, 32, 16], F32), "vp1": ("psum", [128, 32, 16], F32),
+    "zp0": ("psum", [128, 512], F32), "zp1": ("psum", [128, 512], F32),
+}
+DMAS = ["shpA", "shpB", "ofs", "thr", "pic", "exA", "exB", "inc", "rep0", "rep1", "rep2", "cp4", "yi", "ys0", "ys1", "ys2"]
+SENDS = ["ex0A", "ex0B", "in0", "ex1", "ex2", "in1", "in2", "in3", "m1", "m2", "m3"]
+SEMAPHORES = ["eV", "eS", "eP", "eG"] + ["d_" + n for n in DMAS] + ["l_" + n for n in SENDS] + ["r_" + n for n in SENDS]
+
+PRM = dict(CH=[[0, 256, 512], [0, 256, 512], [0, 256, 512], [0, 256, 384, 512]],
+           GE=["SVSVSVSV", "SVSVSVSS", "SVSVSVSS", "SVSVSVSS"], CE=["SSSSVVSS"] * 4,
+           MOD=[512, 256, 0, 0], G1S=[(3, 384)], REP="@ex0B")
+ORDERS = {
+    'V': [40, 17, 15, 16, 34, 19, 18, 56, 57, 41, 36, 20, 21, 58, 35, 38, 37, 67, 69, 59, 44, 43, 60, 61, 46, 115, 117, 123, 90, 89, 121, 125, 119, 93, 94, 95, 96, 102, 97, 98, 103, 99, 104, 100, 39, 101, 155, 42, 107, 137, 138, 157, 141, 106, 142, 105, 143, 144, 108, 145, 109, 146, 111, 147, 110, 201, 177, 178, 205, 148, 211, 209, 181, 149, 182, 207, 183, 184, 188, 185, 186, 189, 187, 190, 239, 192, 197, 193, 223, 224, 241, 227, 191, 228, 229, 194, 230, 231, 232, 195, 233, 196, 285, 261, 295, 262, 289, 234, 265, 235, 266, 291, 267, 293, 268, 269, 272, 270, 271, 273, 322, 275, 277, 276, 308, 307, 324, 311, 274, 312, 313, 278, 314, 279, 315, 316, 280, 317, 281, 371, 344, 377, 345, 318, 379, 373, 348, 319, 349, 357, 350, 358, 375, 362, 351, 361, 359, 352, 360, 353, 363, 366, 382, 383, 364, 354, 365, 407, 408, 367, 355, 386, 368, 387, 411, 388, 412, 413, 414, 389, 390, 416, 391, 417, 392, 418, 393],
+    'S': [32, 28, 22, 30, 24, 26, 23, 33, 27, 29, 66, 68, 75, 73, 71, 77, 84, 80, 86, 82, 114, 88, 25, 31, 116, 134, 128, 130, 132, 154, 136, 156, 161, 163, 159, 172, 165, 168, 174, 170, 200, 176, 203, 202, 218, 220, 216, 214, 238, 222, 240, 249, 243, 247, 245, 252, 256, 258, 254, 284, 260, 286, 287, 298, 300, 302, 304, 321, 306, 323, 330, 328, 326, 332, 339, 341, 337, 335, 370, 343, 396, 395, 404, 402, 398, 400, 381, 406, 415, 419, 394],
+    'P': [74, 72, 76, 70, 45, 83, 79, 85, 81, 78, 122, 87, 124, 120, 118, 91, 92, 133, 127, 129, 131, 126, 135, 162, 160, 139, 158, 140, 171, 164, 167, 169, 173, 166, 175, 204, 210, 208, 179, 180, 206, 217, 219, 215, 213, 212, 221, 248, 242, 225, 226, 246, 244, 251, 255, 253, 257, 250, 259, 294, 288, 263, 264, 290, 292, 297, 299, 301, 303, 296, 305, 329, 327, 309, 310, 325, 331, 338, 336, 340, 334, 333, 342, 376, 372, 378, 346, 347, 403, 401, 374, 397, 399, 380, 405, 384, 385, 409, 410]}
+
+
+def keys(name, a, b, step=64):
+    return ["%s%d" % (name, j) for j in range(a // step, (b + step - 1) // step)]
+
+
+def build(T, topo, core, rank, prm):
+    A, AF = AluOpType, ActivationFunctionType
+    ops = []
+
+    def op(eng, kind, n, fn, r, w, name=None):
+        ops.append(dict(eng=eng, kind=kind, n=n, fn=fn, r=list(r), w=list(w), name=name))
+
+    def V(n, fn, r, w, kind="c"):
+        op("V", kind, n, fn, r, w)
+
+    def dma(name, nbytes, out, in_, r, w, eng="Y"):
+        op(eng, "dma", nbytes, lambda q: q.dma_start(out, in_), r, w, name)
+
+    def send(name, nbytes, hops, out, in_, r, w):
+        dst = T.cores[(rank - hops) % N]
+        rid, pid = topo.addr(dst)[0], topo.addr(dst)[1]
+        mask = topo.mask(core, dst)
+        op("G", "rem", nbytes, lambda q: q.remote_dma(out, in_, T.sem["r_" + name], T.sem["l_" + name], pid, rid, mask), r, [], name)
+        ops[-1]["cnt"] = len(topo.engines(core, dst))
+        op("R", "arr", nbytes, None, [], w, name)
+        ops[-1]["cnt"] = len(topo.engines(T.cores[(rank + hops) % N], core))
+
+    def iota(out, pattern, base, mult, key):
+        n = pattern[0][1] * (pattern[1][1] if len(pattern) > 1 else 1)
+        op("G", "g", n, lambda q: q.iota(out, pattern, base, mult, allow_small_or_imprecise_dtypes=True), [], [key])
+
+    w2 = [T.w20, T.w21, T.w22, T.w23]
+    ft, cp, vp, zp = [T.ft0, T.ft1], [T.cp0, T.cp1], [T.vp0, T.vp1], [T.zp0, T.zp1]
+    mo, mi = [T.mo0, T.mo1, T.mo2, T.mo3], [None, T.mi1, T.mi2, T.mi3, T.mo3]
+    base = [Z0 + SL * t for t in range(5)]
+    slot = [T.w1[:, b + K:b + SL] for b in base]
+    row = 128 * 4
+    idk = ["id%d" % m for m in range(M)]
+    eye = [T.idm[:, 128 * m:128 * m + 128] for m in range(M + 1)]
+
+    dma("ofs", row * 4, T.ofi[:, :], T.ofs[:, :], [], ["ofi"])
+    dma("shpA", row * H, T.w20[:, C:C + H], T.shp[:, 0:H], [], keys("s0", 0, H))
+    dma("pic", 128 * P * 2, T.pw[:, LO:LO + P], T.pic[:, :], [], ["pw"])
+    dma("thr", 128, T.thi[0:8, :], T.thr[:, :], [], ["thi"])
+    dma("shpB", row * H, T.w20[:, C + H:C + F], T.shp[:, H:F], [], keys("s0", H, F))
+    dma("inc", row * C // 2, slot[4], T.inc[:, :], [], ["slot4"])
+    dma("exA", row * C // 2, T.w23[:, 0:C // 2], T.ex[:, 0:C // 2], [], ["ex3A"])
+    dma("exB", row * C // 2, T.w23[:, C // 2:C], T.ex[:, C // 2:C], [], ["ex3B"])
+
+    op("G", "g", 1, lambda q: q.iota(T.pi[:, 0:1], [[0, 1]], 0, 1), [], ["pi"])
+    iota(T.row[:, :], [[1, 144]], 0, 0, "row")
+    iota(T.gi[0:8, :], [[1, 8], [0, 16]], 0, -1, "gi")
+    iota(T.fi[:, 0:32], [[16, 32]], C, 0, "fi")
+    iota(T.fi[:, 32:48], [[SL, 4], [16, 4]], Z0, 0, "fj")
+    iota(T.ki[:, :], [[-16, 4], [1, 64]], 0, 0, "ki")
+    iota(T.big[:, :], [[1, SL]], 0, 0, "big")
+    for j, bits in enumerate((127, 15, 112)):
+        V(1, lambda q, j=j, bits=bits: q.tensor_scalar(T.pj[:, j:j + 1], T.pi[:, 0:1], bits, None, A.bitwise_and), ["pi"], ["pj%d" % j])
+    V(3, lambda q: q.tensor_copy(T.pf[:, 0:3], T.pj[:, 0:3]), ["pj0", "pj1", "pj2"], ["pf"])
+    V(4, lambda q: q.tensor_copy(T.off32[:, :], T.ofi[:, :]), ["ofi"], ["off32"])
+    V(128, lambda q: q.tensor_scalar(eye[0], T.row[:, 0:128], T.pf[:, 0:1], None, A.is_equal), ["row", "pf"], ["id0"])
+    V(144, lambda q: q.tensor_scalar(T.ee[:, :], T.row[:, :], -15.0, T.pf[:, 2:3], A.add, A.is_equal), ["row", "pf"], ["ee"])
+    for m in range(1, M + 1):
+        op("S", "c", 128, lambda q, m=m: q.activation(eye[m], eye[0], AF.Copy, scale=float(2 ** m) if m < M else -1.0), ["id0"], ["id%d" % m])
+    op("S", "c", 144, lambda q: q.activation(T.eh[:, :], T.ee[:, :], AF.Copy, scale=0.5), ["ee"], ["eh"])
+    V(88, lambda q: q.memset(T.one[:, :, :], 1.0), [], ["one"])
+    V(1, lambda q: q.memset(T.cst[:, 0:1], -TINY), [], ["tiny"])
+    V(1, lambda q: q.memset(T.cst[:, 4:5], -7.5), [], ["mid"])
+    V((Z0 + K) // 2, lambda q: q.memset(T.w1[:, 0:Z0 + K], 0.0), [], ["zero"])
+    for t in (1, 2, 3):
+        V(32, lambda q, t=t: q.memset(T.w1[:, base[t]:base[t] + K], 0.0), [], ["spare%d" % t])
+    V(48, lambda q: q.tensor_scalar(T.ff[:, :], T.fi[:, :], T.pf[:, 1:2], None, A.add), ["fi", "fj", "pf"], ["ff"])
+    V(256, lambda q: q.tensor_scalar(T.kc[:, :], T.ki[:, :], T.pf[:, 1:2], None, A.is_equal), ["ki", "pf"], ["kc"])
+    V(128, lambda q: q.tensor_scalar(T.gm[0:8, :], T.gi[0:8, :], 0.0, None, A.is_equal), ["gi"], ["gm"])
+    V(4, lambda q: q.tensor_copy(T.thb[0:8, 0:4], T.thi[0:8, :]), ["thi"], ["thb"])
+    op("P", "mm", [4], lambda q: q.matmul(T.zp1[:, 0:4], T.gm[0:8, :], T.thb[0:8, 0:4], True, True), ["gm", "thb"], ["zp1"])
+    V(4, lambda q: q.tensor_copy(T.thf[:, :], T.zp1[:, 0:4]), ["zp1"], ["thf"])
+
+    send("in0", row * C // 2, 1, slot[0], slot[4], ["slot4"], ["slot0"])
+    send("ex0A", row * C // 2, 1, T.w20[:, 0:C // 2], T.w23[:, 0:C // 2], ["ex3A"], ["ex0A"])
+    send("ex0B", row * C // 2, 1, T.w20[:, C // 2:C], T.w23[:, C // 2:C], ["ex3B"], ["ex0B"])
+    dma("rep1", 128 * P * 2, T.pw[:, LO + P:LO + 2 * P], T.pic[:, :], [prm["REP"]], ["pw1"])
+    dma("rep0", 128 * LO * 2, T.pw[:, 0:LO], T.pic[:, P - LO:P], [], ["pw0"])
+    dma("rep2", 128 * LO * 2, T.pw[:, LO + 2 * P:PW], T.pic[:, 0:LO], [], ["pw2"])
+
+    def probes(t, f0, f1):
+        x = min(max(prm["MOD"][t], f0), f1)
+        if x > f0:
+            s, n = w2[t][:, C + f0:C + x], x - f0
+            V(n, lambda q: q.tensor_scalar(T.xi[:, f0:x], s, T.off32[:, t:t + 1], None, A.add), keys("s%d" % t, f0, x) + ["off32"], keys("xi", f0, x))
+            V(n, lambda q: q.tensor_scalar(T.xj[:, f0:x], T.xi[:, f0:x], P - 1, None, A.bitwise_and), keys("xi", f0, x), keys("xj", f0, x))
+            V(n, lambda q: q.tensor_copy(T.off[:, f0:x], T.xj[:, f0:x]), keys("xj", f0, x), keys("off", f0, x))
+        if f1 > x:
+            V(f1 - x, lambda q: q.tensor_scalar(T.off[:, x:f1], w2[t][:, C + x:C + f1], T.off32[:, t:t + 1], float(LO), A.add, A.add),
+              keys("s%d" % t, x, f1) + ["off32"], keys("off", x, f1))
+
+    def patch(t):
+        V(4, lambda q: q.tensor_scalar(T.tl[:, :], mi[t][:, K:K + 4], float(-base[t - 1]), None, A.add), ["mi%d" % t], ["tl"])
+        V(K, lambda q: q.tensor_copy(T.w1[:, base[t]:base[t] + SL].indirect(T.tl[:, :]), mi[t][:, 0:K]),
+          ["tl", "mi%d" % t, "mh%d" % t], ["slot%d" % t, "spare%d" % t], "sca")
+
+    def gather(t, a):
+        mod = a < prm["MOD"][t]
+        src = (T.pw[:, LO:LO + P] if mod else T.pw[:, :]).indirect(T.off[:, a:a + 64])
+        r = (["pw"] if mod else ["pw", "pw0", "pw1", "pw2"]) + keys("off", a, a + 64)
+        out = T.u[:, 16 * a:16 * a + 1024]
+        if prm["GE"][t][a // 64] == "V":
+            op("V", "gat", 1024, lambda q: q.tensor_copy(out, src), r, ["u%d" % a])
+        else:
+            op("S", "gat", 1024, lambda q: q.activation(out, src, AF.Copy), r, ["u%d" % a])
+
+    def compare(t, a, j):
+        d, eng = 5 - t, prm["CE"][t][a // 64]
+        for h, (m0, m1) in enumerate(((0, 8), (8, M))):
+            ps, out, pk = cp[j][:, 64 * h:64 * h + 64, 0:m1 - m0], T.cmp[:, a:a + 64, m0:m1], "cp%d%d" % (j, h)
+
+            def fill(q, h=h, m0=m0, m1=m1):
+                for m in range(m0, m1):
+                    o = cp[j][:, 64 * h:64 * h + 64, m - m0]
+                    q.matmul(o, eye[0], T.u[:, 16 * a + m:16 * a + 1024:16], True, False)
+                    ins = q.matmul(o, eye[M], T.u[:, 16 * a + m + d:16 * a + 1024:16], False, True)
+                return ins
+            n = 64 * (m1 - m0)
+            op("P", "mm", [n, n], fill, ["id0", "id%d" % M, "u%d" % a], [pk])
+            ck = ["cmp%d_%d" % (a // 64, h)]
+            if eng == "S":
+                op("S", "c", n, lambda q, ps=ps, out=out: q.activation(out, ps, AF.Sign, bias=T.cst[:, 0:1]), [pk, "tiny"], ck)
+            else:
+                V(n, lambda q, ps=ps, out=out: q.tensor_scalar(out, ps, 0.0, None, A.is_gt), [pk], ck)
+
+    def votes(t, c, f0, x, y):
+        sign = prm["CE"][t][x // 64] == "S"
+        out = vp[c][:, (x - f0) // 16:(y - f0) // 16, 0:M]
+
+        def fn(q):
+            if sign:
+                q.matmul(out, eye[3], T.one[:, 0:(y - x) // 16, :], True, False)
+            for b in range(16):
+                ins = q.matmul(out, (T.eh if sign else T.ee)[:, 15 - b:143 - b], T.cmp[:, x + b:y:16, :], b == 0 and not sign, b == 15)
+            return ins
+        op("P", "mm", [(y - x) // 16 * M] * (17 if sign else 16), fn,
+           ["ee", "eh", "one", "id3"] + ["cmp%d_%d" % (z, h) for z in range(x // 64, y // 64) for h in (0, 1)], ["vp%d" % c])
+
+    def tail(t, c, f0, f1, nys):
+        n, na, a0 = f1 - f0, (f1 - f0) // 16, f0 // 16
+        vk, fk, cnt = "vp%d" % c, ["ft%d%d" % (c, j) for j in range(3)], vp[c][:, 0:na, 0:M]
+        fs = [ft[c][:, 16 * j:16 * j + na, :] for j in range(3)]
+        op("S", "c", na * M, lambda q: q.activation(fs[0], cnt, AF.Abs, bias=T.cst[:, 4:5]), ["mid"], [fk[0], vk])
+        V(na * M, lambda q: q.tensor_scalar(fs[2], cnt, 9.0, None, A.is_ge), [vk], [fk[2]])
+        V(na * M // 2, lambda q: q.tensor_scalar(fs[1], fs[0], 4.0, None, A.is_ge), [fk[0]], [fk[1]])
+
+        def sums(q, j):
+            for m in range(M):
+                if j == 1:
+                    ins = q.matmul(zp[c][:, 0:na], eye[0], ft[c][:, 16:16 + na, m], m == 0, m == M - 1)
+                else:
+                    ins = q.matmul(zp[c][:, 16:16 + na], eye[m], ft[c][:, 32:32 + na, m], m == 0, m == M - 1)
+            return ins
+        for j in (2, 1):
+            op("P", "mm", [na] * M, lambda q, j=j: sums(q, j), [fk[j]] + idk, ["zp%d" % c])
+        ub, t2, t3 = T.ub[:, a0:a0 + na], T.tb[:, 2 * a0:2 * a0 + na], T.tb[:, 2 * a0 + na:2 * a0 + 2 * na]
+        kub, kt, ku, kil, kup = keys("ub", f0, f1), keys("ta", f0, f1), keys("tb", f0, f1), keys("il", f0, f1), keys("up", f0, f1)
+        V(na, lambda q: q.tensor_scalar(ub, zp[c][:, 0:na], T.thf[:, t:t + 1], float(base[t] + K), A.is_ge, A.mult), ["zp%d" % c, "thf"], kub)
+        V(na, lambda q: q.tensor_tensor(t2, zp[c][:, 16:16 + na], ub, A.add), ["zp%d" % c] + kub, kt + ku)
+        V(2 * na, lambda q: q.tensor_tensor(t3, t2, T.ff[:, a0:a0 + na], A.min), kt + ["ff"], ku)
+        V(2 * na, lambda q: q.tensor_copy(T.il[:, 2 * a0:2 * a0 + 2 * na], T.tb[:, 2 * a0:2 * a0 + 2 * na]), kt + ku, kil)
+        r = ["zero"] + ["slot%d" % j for j in range(t + 1)] + ["spare%d" % j for j in range(1, t + 1)] + kil
+        src = T.w1[:, 0:base[t] + SL].indirect(T.il[:, 2 * a0:2 * a0 + na])
+        if (t, f0) in prm["G1S"]:
+            op("S", "gat", n, lambda q: q.activation(T.up[:, f0:f1], src, AF.Copy), r, kup)
+        else:
+            op("V", "gat", n, lambda q: q.tensor_copy(T.up[:, f0:f1], src), r, kup)
+        new, nk = (w2[t + 1][:, C + f0:C + f1], keys("s%d" % (t + 1), f0, f1)) if t < 3 else (T.xi[:, f0:f1], keys("xi", f0, f1))
+        op("V", "gat", n, lambda q: q.tensor_tensor(new, w2[t][:, :].indirect(T.il[:, 2 * a0 + na:2 * a0 + 2 * na]), T.up[:, f0:f1], A.add),
+           ["ex%dA" % t, "ex%dB" % t] + keys("s%d" % t, 0, F) + kil + kup, nk)
+        if t < 3:
+            probes(t + 1, f0, f1)
+        else:
+            V(n, lambda q: q.tensor_scalar(T.xj[:, f0:f1], T.xi[:, f0:f1], P - 1, None, A.bitwise_and), nk, keys("xj", f0, f1))
+            V(n, lambda q: q.tensor_copy(T.yf[:, f0:f1], T.xj[:, f0:f1]), keys("xj", f0, f1), keys("yf", f0, f1))
+            dma("ys%d" % nys, row * n, T.ys[:, f0:f1], T.yf[:, f0:f1], keys("yf", f0, f1), [], "S" if nys else "Y")
+        if f0 <= K * t < f1:
+            halve(t, T.tb[:, a0 + 4 * t:a0 + 4 * t + 4], kt, kup)
+
+    def halve(t, t2, kt, kup):
+        spare = T.ff[:, 32 + 4 * t:36 + 4 * t]
+        mk, hk = ("mo%d" % t, "mg%d" % t) if t < 3 else ("mi4", "mh4")
+        V(8, lambda q: q.tensor_tensor(T.y0[:, :], t2, spare, A.max), kt + ["ff"], ["y0"])
+        V(4, lambda q: q.tensor_scalar(T.yl[:, :], T.y0[:, :], float(-base[t]), None, A.add), ["y0"], ["yl"])
+        for a in range(4):
+            op("V", "gat", K, lambda q, a=a: q.tensor_scalar(T.ne[:, K * a:K * a + K], T.big[:, :].indirect(T.yl[:, :]), float(base[t]), T.y0[:, a:a + 1], A.add, A.not_equal),
+               ["big", "yl", "y0"], ["ne%d" % a])
+        V(128, lambda q: q.tensor_tensor_scan(T.kp[:, :], T.ne[:, :], T.kc[:, :], 0.0, A.mult, A.max), ["ne0", "ne1", "ne2", "ne3", "kc"], ["kp"])
+        V(8, lambda q: q.tensor_tensor(T.ym[:, :], T.kp[:, K - 1::K], T.y0[:, :], A.mult), ["kp", "y0"], ["ym"])
+        V(8, lambda q: q.tensor_tensor(mo[t][:, K:K + 4], T.ym[:, :], spare, A.max), ["ym", "ff"], [mk])
+        V(K, lambda q: q.tensor_scalar(mo[t][:, 0:K], T.up[:, K * t:K * t + K], 0.5, -0.25, A.mult, A.add), kup, [hk])
+        if t < 3:
+            send("m%d" % (t + 1), row * 68, 1, mi[t + 1][:, :], mo[t][:, :], [mk, hk], ["mi%d" % (t + 1), "mh%d" % (t + 1)])
+        else:
+            patch(4)
+            dma("yi", row * C // 2, T.yi[:, :], slot[4], ["slot4"], [])
+
+    probes(0, 0, H)
+    probes(0, H, F)
+    ncp, nch = 0, 0
+    for t in range(NT):
+        if t > 0:
+            patch(t)
+        if t < 3:
+            send("in%d" % (t + 1), row * C // 2, 1, slot[t + 1], slot[t], ["slot%d" % t], ["slot%d" % (t + 1)])
+        else:
+            dma("cp4", row * C // 2, slot[4], slot[3], ["slot3"], ["slot4"])
+        if t < 2:
+            send("ex%d" % (t + 1), row * C, t + 2, w2[t + 1][:, 0:C], T.w23[:, 0:C], ["ex3A", "ex3B", "slot%d" % t], ["ex%dA" % (t + 1), "ex%dB" % (t + 1)])
+        ch = prm["CH"][t]
+        for nys, (f0, f1) in enumerate(zip(ch[:-1], ch[1:])):
+            for a in range(f0, f1, 64):
+                gather(t, a)
+            for a in range(f0, f1, 64):
+                compare(t, a, ncp % 2)
+                ncp += 1
+                if a % 128:
+                    votes(t, nch % 2, f0, a - 64, a + 64)
+            tail(t, nch % 2, f0, f1, nys)
+            nch += 1
+    return ops
+
+
+def link(ops):
+    last, readers, sends = {}, {}, {}
+    for i, o in enumerate(ops):
+        deps = set()
+        if o["kind"] == "rem":
+            sends[o["name"]] = i
+        if o["kind"] == "arr":
+            o["src"] = sends[o["name"]]
+        for key in o["r"]:
+            if key[0] == "@":
+                deps.add(sends[key[1:]])
+            elif key in last:
+                deps.add(last[key])
+        if o["kind"] != "arr":
+            for key in o["w"]:
+                if key in last:
+                    deps.add(last[key])
+                deps.update(readers.get(key, []))
+        for key in o["r"]:
+            readers.setdefault(key, []).append(i)
+        for key in o["w"]:
+            last[key] = i
+            readers[key] = []
+        deps.discard(i)
+        o["deps"] = sorted(deps)
+
+
+def rank_program(g, core, T, topo):
+    rank = T.rank_of(core)
+    if rank is None:
+        return
+    ops = build(T, topo, core, rank, PRM)
+    link(ops)
+    order = {e: [i for i, o in enumerate(ops) if o["eng"] == e] for e in "GY"}
+    order.update(ORDERS)
+    queue = {"V": g.vector, "S": g.scalar, "P": g.tensor, "G": g, "Y": g.sync}
+    needed = set()
+    for o in ops:
+        for j in o["deps"]:
+            if not (o["eng"] == "P" and ops[j]["eng"] == "P"):
+                needed.add(j)
+    mark = {}
+    for e in "VSPG":
+        cnt = 0
+        for i in order[e]:
+            if ops[i]["kind"] not in ("rem", "dma") and i in needed:
+                cnt += 1
+                mark[i] = ("e" + e, cnt)
+    for i, o in enumerate(ops):
+        if o["kind"] == "dma":
+            mark[i] = ("d_" + o["name"], 16)
+        elif o["kind"] == "rem":
+            mark[i] = ("l_" + o["name"], o["cnt"])
+        elif o["kind"] == "arr":
+            mark[i] = ("r_" + o["name"], o["cnt"])
+    top = {}
+    for e in "SGVPY":
+        q, seen = queue[e], {}
+        for i in order[e]:
+            o = ops[i]
+            want = {}
+            for j in o["deps"]:
+                if e == "P" and ops[j]["eng"] == "P":
+                    continue
+                s, v = mark[j]
+                want[s] = max(want.get(s, 0), v)
+            for s in sorted(want):
+                if want[s] > seen.get(s, 0):
+                    q.wait_ge(T.sem[s], want[s])
+                    seen[s] = want[s]
+                    top[s] = max(top.get(s, 0), want[s])
+            ins = o["fn"](q)
+            if o["kind"] == "dma":
+                ins.then_inc(T.sem[mark[i][0]], 16)
+            elif o["kind"] != "rem" and i in mark:
+                ins.then_inc(T.sem[mark[i][0]], 1)
+    end = {}
+    for s, v in mark.values():
+        end[s] = max(end.get(s, 0), v)
+    for s in sorted(end):
+        if end[s] > top.get(s, 0):
+            g.sync.wait_ge(T.sem[s], end[s])

@@ -1,65 +1,108 @@
-from concourse.mybir import AluOpType, ActivationFunctionType
+from concourse.mybir import AluOpType, ActivationFunctionType, AxisListType
 
 N, P, F, M, C, NT, K = 4, 4096, 512, 11, 2048, 4, 64
 H = F // 2
 LO = 768
 PW = LO + 2 * P + LO
-Z0 = C + F
-SL = K + C
+Z = 16
+SL = Z + K + C
+SURE = 4096.0
+X0 = SURE - Z - K
 TINY = 2.0 ** -108
 BF, F32, I32, U16 = "bfloat16", "float32", "int32", "uint16"
 
+ROWS = [([6, 7, 8, 9], [0, 5, 10, 15]), ([4, 5, 6, 7], [7, 8, 9, 10]), ([3, 4, 9, 10], [2, 5, 8, 11]), ([2, 6, 10, 3], [5, 7, 9, 11])]
+RIGHT = [0, 1, 0, 0]
+
 SCRATCH = {
-    "pw": ("sbuf", [128, PW], BF), "u": ("sbuf", [128, F * 16], BF), "cmp": ("sbuf", [128, F, M], BF),
-    "w1": ("sbuf", [128, Z0 + 5 * SL], BF),
+    "pw": ("sbuf", [128, PW], BF), "u": ("sbuf", [128, F * 8], BF), "cl": ("sbuf", [128, F * 4], BF), "cr": ("sbuf", [128, F * 4], BF),
+    "sg": ("sbuf", [128, 3, F], BF), "w1": ("sbuf", [128, 5, SL], BF),
     "w20": ("sbuf", [128, C + F], I32), "w21": ("sbuf", [128, C + F], I32),
     "w22": ("sbuf", [128, C + F], I32), "w23": ("sbuf", [128, C + F], I32),
-    "xi": ("sbuf", [128, F], I32), "xj": ("sbuf", [128, F], I32), "yf": ("sbuf", [128, F], F32), "off": ("sbuf", [128, F], U16),
-    "up": ("sbuf", [128, F], BF),
-    "ft0": ("sbuf", [128, 48, M], BF), "ft1": ("sbuf", [128, 48, M], BF), "one": ("sbuf", [128, 16, M], BF),
-    "ub": ("sbuf", [128, 32], F32), "tb": ("sbuf", [128, 64], F32), "il": ("sbuf", [128, 64], U16),
-    "ofi": ("sbuf", [128, 4], I32), "off32": ("sbuf", [128, 4], F32),
+    "xi": ("sbuf", [128, F], I32), "xj": ("sbuf", [128, F], I32), "xf": ("sbuf", [128, 4 * NT, H + 4], F32), "yf": ("sbuf", [128, F], F32),
+    "ov": ("sbuf", [128, F // 2], U16), "oc": ("sbuf", [128, F // 2], U16), "up": ("sbuf", [128, F], F32),
+    "ab": ("sbuf", [128, F], BF), "ft": ("sbuf", [128, 2, F], BF),
+    "ub": ("sbuf", [128, 32], F32), "ta": ("sbuf", [128, 32], F32), "tb": ("sbuf", [128, 32], F32),
+    "ia": ("sbuf", [128, 32], U16), "ib": ("sbuf", [128, 32], U16),
+    "ofi": ("sbuf", [128, 4], I32), "ofs32": ("sbuf", [128, 4], F32), "ob": ("sbuf", [128, 4], F32), "oh": ("sbuf", [128, 4], F32),
     "thi": ("sbuf", [128, 4], I32), "thb": ("sbuf", [128, 8], BF), "thf": ("sbuf", [128, 4], F32),
-    "row": ("sbuf", [128, 144], F32), "big": ("sbuf", [128, SL], F32), "cst": ("sbuf", [128, 8], F32),
+    "row": ("sbuf", [128, 144], F32), "row3": ("sbuf", [128, 8, 16], F32), "big": ("sbuf", [128, SL], F32), "cst": ("sbuf", [128, 8], F32),
     "pi": ("sbuf", [128, 4], I32), "pj": ("sbuf", [128, 4], I32), "pf": ("sbuf", [128, 4], F32),
     "gi": ("sbuf", [128, 128], F32), "gm": ("sbuf", [128, 128], BF),
-    "ee": ("sbuf", [128, 144], BF), "eh": ("sbuf", [128, 144], BF), "idm": ("sbuf", [128, (M + 1) * 128], BF),
-    "fi": ("sbuf", [128, 48], F32), "ff": ("sbuf", [128, 48], F32),
+    "ee": ("sbuf", [128, 144], BF), "eh": ("sbuf", [128, 144], BF), "ew": ("sbuf", [128, 144], BF), "idm": ("sbuf", [128, 256], BF),
+    "id3": ("sbuf", [128, 8, 16], F32), "sv": ("sbuf", [128, 4 * 17, 8], F32), "sc": ("sbuf", [128, 8 * 35, 4], F32),
+    "m16": ("sbuf", [128, 16], F32), "p2": ("sbuf", [128, 64], F32), "pm": ("sbuf", [128, 32], F32), "pc": ("sbuf", [128, 4], F32),
+    "ind": ("sbuf", [128, 4], F32), "ba": ("sbuf", [128, 4], F32), "bs": ("sbuf", [128, 4], F32),
+    "fi": ("sbuf", [128, 40], F32), "ff": ("sbuf", [128, 36], F32),
     "ki": ("sbuf", [128, 256], F32), "kc": ("sbuf", [128, 256], BF),
     "y0": ("sbuf", [128, 4], F32), "yl": ("sbuf", [128, 4], U16), "ne": ("sbuf", [128, 256], BF),
     "kp": ("sbuf", [128, 256], BF), "ym": ("sbuf", [128, 4], F32), "tl": ("sbuf", [128, 4], U16),
     "mo0": ("sbuf", [128, 68], I32), "mo1": ("sbuf", [128, 68], I32), "mo2": ("sbuf", [128, 68], I32), "mo3": ("sbuf", [128, 68], I32),
     "mi1": ("sbuf", [128, 68], I32), "mi2": ("sbuf", [128, 68], I32), "mi3": ("sbuf", [128, 68], I32),
-    "cp0": ("psum", [128, 128, 8], F32), "cp1": ("psum", [128, 128, 8], F32),
-    "vp0": ("psum", [128, 32, 16], F32), "vp1": ("psum", [128, 32, 16], F32),
-    "zp0": ("psum", [128, 512], F32), "zp1": ("psum", [128, 512], F32),
+    "lv": ("psum", [128, 512], F32), "lc": ("psum", [128, 512], F32),
+    "dp0": ("psum", [128, 4, 128], F32), "dp1": ("psum", [128, 4, 128], F32),
+    "vp0": ("psum", [128, 512], F32), "vp1": ("psum", [128, 512], F32),
+    "zp0": ("psum", [128, 2, 256], F32), "zp1": ("psum", [128, 2, 256], F32),
 }
-DMAS = ["shpA", "shpB", "ofs", "thr", "pic", "exA", "exB", "inc", "rep0", "rep1", "rep2", "cp4", "yi", "ys0", "ys1", "ys2"]
+BANKS = [n for n in SCRATCH if SCRATCH[n][0] == "psum"]
+DMAS = ["shpA", "shpB", "ofs", "thr", "pic", "exA", "exB", "inc", "rep0", "rep3", "rep1", "rep2", "cp4", "yi", "ys0", "ys1", "ys2", "ys3"]
 SENDS = ["ex0A", "ex0B", "in0", "ex1", "ex2", "in1", "in2", "in3", "m1", "m2", "m3"]
 SEMAPHORES = ["eV", "eS", "eP", "eG"] + ["d_" + n for n in DMAS] + ["l_" + n for n in SENDS] + ["r_" + n for n in SENDS]
 
-PRM = dict(CH=[[0, 256, 512], [0, 256, 512], [0, 256, 512], [0, 256, 384, 512]],
-           GE=["SVSVSVSV", "SVSVSVSS", "SVSVSVSS", "SVSVSVSS"], CE=["SSSSVVSS"] * 4,
-           MOD=[512, 256, 0, 0], G1S=[(3, 384)], REP="@ex0B")
-ORDERS = {
-    'V': [40, 17, 15, 16, 34, 19, 18, 56, 57, 41, 36, 20, 21, 58, 35, 38, 37, 67, 69, 59, 44, 43, 60, 61, 46, 115, 117, 123, 90, 89, 121, 125, 119, 93, 94, 95, 96, 102, 97, 98, 103, 99, 104, 100, 39, 101, 155, 42, 107, 137, 138, 157, 141, 106, 142, 105, 143, 144, 108, 145, 109, 146, 111, 147, 110, 201, 177, 178, 205, 148, 211, 209, 181, 149, 182, 207, 183, 184, 188, 185, 186, 189, 187, 190, 239, 192, 197, 193, 223, 224, 241, 227, 191, 228, 229, 194, 230, 231, 232, 195, 233, 196, 285, 261, 295, 262, 289, 234, 265, 235, 266, 291, 267, 293, 268, 269, 272, 270, 271, 273, 322, 275, 277, 276, 308, 307, 324, 311, 274, 312, 313, 278, 314, 279, 315, 316, 280, 317, 281, 371, 344, 377, 345, 318, 379, 373, 348, 319, 349, 357, 350, 358, 375, 362, 351, 361, 359, 352, 360, 353, 363, 366, 382, 383, 364, 354, 365, 407, 408, 367, 355, 386, 368, 387, 411, 388, 412, 413, 414, 389, 390, 416, 391, 417, 392, 418, 393],
-    'S': [32, 28, 22, 30, 24, 26, 23, 33, 27, 29, 66, 68, 75, 73, 71, 77, 84, 80, 86, 82, 114, 88, 25, 31, 116, 134, 128, 130, 132, 154, 136, 156, 161, 163, 159, 172, 165, 168, 174, 170, 200, 176, 203, 202, 218, 220, 216, 214, 238, 222, 240, 249, 243, 247, 245, 252, 256, 258, 254, 284, 260, 286, 287, 298, 300, 302, 304, 321, 306, 323, 330, 328, 326, 332, 339, 341, 337, 335, 370, 343, 396, 395, 404, 402, 398, 400, 381, 406, 415, 419, 394],
-    'P': [74, 72, 76, 70, 45, 83, 79, 85, 81, 78, 122, 87, 124, 120, 118, 91, 92, 133, 127, 129, 131, 126, 135, 162, 160, 139, 158, 140, 171, 164, 167, 169, 173, 166, 175, 204, 210, 208, 179, 180, 206, 217, 219, 215, 213, 212, 221, 248, 242, 225, 226, 246, 244, 251, 255, 253, 257, 250, 259, 294, 288, 263, 264, 290, 292, 297, 299, 301, 303, 296, 305, 329, 327, 309, 310, 325, 331, 338, 336, 340, 334, 333, 342, 376, 372, 378, 346, 347, 403, 401, 374, 397, 399, 380, 405, 384, 385, 409, 410]}
+LAG = dict(And=-3.5, KP=-1, MG=-0.5, MO=-6, NE=6, Or=-6, SCA=-5.5, TL=-6, YM=-5, ab1=0, cl2=-3, cl3=1.5, cr2=6, cr3=1, df2=-1, df3=1.5, fb1=0.5,
+           fe1=-0.5, ia=-5, ib=-6, kp=-3.5, ll=-0.5, lr=-2, lv=-4, mg=6, mo=4, ne=6, ol=6, ov=1.5, sc=-1, sc4=-5, sca=0, sg2=-4.5, sg3=-3.5,
+           sm=5, ta=-5.5, tb=-3.5, tl=4.5, u2=1.5, u3=6, ub=-5.5, up=-3.5, vt2=5, vt3=0, x1=0.5, xf=0.5, yf=-2, ym=6)
+PRM = dict(LAG=LAG, SEL=[0, 0, 1], GP=2560, FS=False, NE="SSVV", SC="G", CH=[[0, 96, 192], [192, 272, 352], [352, 432, 512]])
 
 
-def keys(name, a, b, step=64):
+def keys(name, a, b, step=16):
     return ["%s%d" % (name, j) for j in range(a // step, (b + step - 1) // step)]
+
+
+def runs(lm):
+    out, k = [], 0
+    while k < len(lm):
+        n, st = 1, 1
+        if k + 1 < len(lm) and lm[k + 1] > lm[k]:
+            st = lm[k + 1] - lm[k]
+            while k + n < len(lm) and lm[k + n] - lm[k + n - 1] == st:
+                n += 1
+        out.append((k, n, lm[k], st))
+        k += n
+    return out
+
+
+def plan(t):
+    d, rows = 5 - t, ROWS[t]
+    left, right = [q - d for q in rows[0]], [q + d for q in rows[RIGHT[t]]]
+    place = {}
+    for w in (1, 0):
+        for k, q in enumerate(rows[w]):
+            place[q] = 2 * k + w
+    rest = [m for m in range(M) if m not in left and m not in rows[RIGHT[t]]]
+    return left, right, [(m, place[m], place[m + d]) for m in rest]
 
 
 def build(T, topo, core, rank, prm):
     A, AF = AluOpType, ActivationFunctionType
-    ops = []
+    ops, now, count, ch = [], [-9], [0], prm["CH"]
+    nc = len(ch)
+    mine = [(4 * nc, "tl"), (4 * nc, "sca")] + [(3 * nc + c, x) for c in range(nc) for x in "ne kp ym mo mg".split()]
 
-    def op(eng, kind, n, fn, r, w, name=None):
-        ops.append(dict(eng=eng, kind=kind, n=n, fn=fn, r=list(r), w=list(w), name=name))
+    def op(eng, kind, n, fn, r, w, name=None, tag=None):
+        if (now[0], tag) in mine:
+            tag = tag.upper()
+        ops.append(dict(eng=eng, kind=kind, n=n, fn=fn, r=list(r), w=list(w), name=name, chunk=now[0], tag=tag))
 
-    def V(n, fn, r, w, kind="c"):
-        op("V", kind, n, fn, r, w)
+    def V(n, fn, r, w, tag=None, kind="c"):
+        op("V", kind, n, fn, r, w, None, tag)
+
+    def S(n, fn, r, w, tag=None, kind="c"):
+        op("S", kind, n, fn, r, w, None, tag)
+
+    def PE(n, fn, r, w, tag=None, passes=1):
+        op("P", "mm", n, fn, r, w, None, tag)
+        ops[-1]["w4"] = passes
 
     def dma(name, nbytes, out, in_, r, w, eng="Y"):
         op(eng, "dma", nbytes, lambda q: q.dma_start(out, in_), r, w, name)
@@ -78,208 +121,271 @@ def build(T, topo, core, rank, prm):
         op("G", "g", n, lambda q: q.iota(out, pattern, base, mult, allow_small_or_imprecise_dtypes=True), [], [key])
 
     w2 = [T.w20, T.w21, T.w22, T.w23]
-    ft, cp, vp, zp = [T.ft0, T.ft1], [T.cp0, T.cp1], [T.vp0, T.vp1], [T.zp0, T.zp1]
+    dp, vp, zp = [T.dp0, T.dp1], [T.vp0, T.vp1], [T.zp0, T.zp1]
     mo, mi = [T.mo0, T.mo1, T.mo2, T.mo3], [None, T.mi1, T.mi2, T.mi3, T.mo3]
-    base = [Z0 + SL * t for t in range(5)]
-    slot = [T.w1[:, b + K:b + SL] for b in base]
+    slot = [T.w1[:, t, Z + K:SL] for t in range(5)]
     row = 128 * 4
-    idk = ["id%d" % m for m in range(M)]
-    eye = [T.idm[:, 128 * m:128 * m + 128] for m in range(M + 1)]
+    eye, neg = T.idm[:, 0:128], T.idm[:, 128:256]
+    plans = [plan(t) for t in range(NT)]
+    own, low, grp = T.pf[:, 0:1], T.pf[:, 1:2], T.pf[:, 2:3]
+    selk = [[["sel%d_%d_%d" % (t, j, r[0]) for r in runs(lm)] for j, lm in enumerate(ROWS[t] + plans[t][0:2])] for t in range(NT)]
 
+    def select(t):
+        for j, lm in enumerate(ROWS[t] + plans[t][0:2]):
+            for k, n, a, st in runs(lm):
+                if j < 2:
+                    out = T.sv[:, 17 * t + 1:17 * t + 17:2, 2 * k + j:2 * (k + n - 1) + j + 1:2]
+                else:
+                    out = T.sc[:, 35 * (2 * t + j - 2) + 3:35 * (2 * t + j - 1):4, k:k + n]
+                src = T.id3[:, :, a:a + st * (n - 1) + 1:st]
+                S(8 * n, lambda q, out=out, src=src: q.activation(out, src, AF.Copy), ["id3", "selv%d" % min(t, 1), "selc%d" % min(t, 1)], ["sel%d_%d_%d" % (t, j, k)])
+
+    def first(c, tag=None):
+        f0, f1 = ch[c][0], ch[c][-1]
+        n = f1 - f0
+        V(n, lambda q: q.tensor_scalar(T.xi[:, f0:f1], T.w20[:, C + f0:C + f1], T.ofs32[:, 0:1], None, A.add), keys("s0", f0, f1) + ["ofs32"], keys("xi", f0, f1), tag)
+        V(n, lambda q: q.tensor_scalar(T.xj[:, f0:f1], T.xi[:, f0:f1], P - 1, None, A.bitwise_and), keys("xi", f0, f1), keys("xj", f0, f1), tag)
+        V(n, lambda q: q.tensor_copy(T.xf[:, c, 4:4 + n], T.xj[:, f0:f1]), keys("xj", f0, f1), ["xf%d" % c], tag)
+
+    H = ch[0][-1]
     dma("ofs", row * 4, T.ofi[:, :], T.ofs[:, :], [], ["ofi"])
-    dma("shpA", row * H, T.w20[:, C:C + H], T.shp[:, 0:H], [], keys("s0", 0, H))
+    dma("shpA", row * H, T.w20[:, C:C + H], T.shp[:, 0:H], [], keys("s0", 0, H), "S")
     dma("pic", 128 * P * 2, T.pw[:, LO:LO + P], T.pic[:, :], [], ["pw"])
-    dma("thr", 128, T.thi[0:8, :], T.thr[:, :], [], ["thi"])
     dma("shpB", row * H, T.w20[:, C + H:C + F], T.shp[:, H:F], [], keys("s0", H, F))
+    dma("thr", 128, T.thi[0:8, :], T.thr[:, :], [], ["thi"])
     dma("inc", row * C // 2, slot[4], T.inc[:, :], [], ["slot4"])
     dma("exA", row * C // 2, T.w23[:, 0:C // 2], T.ex[:, 0:C // 2], [], ["ex3A"])
     dma("exB", row * C // 2, T.w23[:, C // 2:C], T.ex[:, C // 2:C], [], ["ex3B"])
 
     op("G", "g", 1, lambda q: q.iota(T.pi[:, 0:1], [[0, 1]], 0, 1), [], ["pi"])
-    iota(T.row[:, :], [[1, 144]], 0, 0, "row")
+    iota(T.row3[:, :, :], [[1, 128]], 0, 0, "row3")
+    iota(T.row[:, :], [[1, 144]], -15, 0, "row")
     iota(T.gi[0:8, :], [[1, 8], [0, 16]], 0, -1, "gi")
     iota(T.fi[:, 0:32], [[16, 32]], C, 0, "fi")
-    iota(T.fi[:, 32:48], [[SL, 4], [16, 4]], Z0, 0, "fj")
+    iota(T.fi[:, 32:36], [[16, 4]], int(X0) + Z, 0, "fj")
+    iota(T.fi[:, 36:39], [[256, 3]], 256, 0, "fk")
+    iota(T.big[:, 0:SL // 4], [[1, SL // 4]], int(X0), 0, "big0")
     iota(T.ki[:, :], [[-16, 4], [1, 64]], 0, 0, "ki")
-    iota(T.big[:, :], [[1, SL]], 0, 0, "big")
+    V(136, lambda q: q.memset(T.sv[:, 0:17, :], 0.0), [], ["selv0"])
+    V(280, lambda q: q.memset(T.sc[:, 0:70, :], 0.0), [], ["selc0"])
     for j, bits in enumerate((127, 15, 112)):
         V(1, lambda q, j=j, bits=bits: q.tensor_scalar(T.pj[:, j:j + 1], T.pi[:, 0:1], bits, None, A.bitwise_and), ["pi"], ["pj%d" % j])
-    V(3, lambda q: q.tensor_copy(T.pf[:, 0:3], T.pj[:, 0:3]), ["pj0", "pj1", "pj2"], ["pf"])
-    V(4, lambda q: q.tensor_copy(T.off32[:, :], T.ofi[:, :]), ["ofi"], ["off32"])
-    V(128, lambda q: q.tensor_scalar(eye[0], T.row[:, 0:128], T.pf[:, 0:1], None, A.is_equal), ["row", "pf"], ["id0"])
-    V(144, lambda q: q.tensor_scalar(T.ee[:, :], T.row[:, :], -15.0, T.pf[:, 2:3], A.add, A.is_equal), ["row", "pf"], ["ee"])
-    for m in range(1, M + 1):
-        op("S", "c", 128, lambda q, m=m: q.activation(eye[m], eye[0], AF.Copy, scale=float(2 ** m) if m < M else -1.0), ["id0"], ["id%d" % m])
-    op("S", "c", 144, lambda q: q.activation(T.eh[:, :], T.ee[:, :], AF.Copy, scale=0.5), ["ee"], ["eh"])
-    V(88, lambda q: q.memset(T.one[:, :, :], 1.0), [], ["one"])
     V(1, lambda q: q.memset(T.cst[:, 0:1], -TINY), [], ["tiny"])
-    V(1, lambda q: q.memset(T.cst[:, 4:5], -7.5), [], ["mid"])
-    V((Z0 + K) // 2, lambda q: q.memset(T.w1[:, 0:Z0 + K], 0.0), [], ["zero"])
-    for t in (1, 2, 3):
-        V(32, lambda q, t=t: q.memset(T.w1[:, base[t]:base[t] + K], 0.0), [], ["spare%d" % t])
-    V(48, lambda q: q.tensor_scalar(T.ff[:, :], T.fi[:, :], T.pf[:, 1:2], None, A.add), ["fi", "fj", "pf"], ["ff"])
-    V(256, lambda q: q.tensor_scalar(T.kc[:, :], T.ki[:, :], T.pf[:, 1:2], None, A.is_equal), ["ki", "pf"], ["kc"])
+    V(3, lambda q: q.tensor_copy(T.pf[:, 0:3], T.pj[:, 0:3]), ["pj0", "pj1", "pj2"], ["pf"])
+    V(8, lambda q: q.memset(T.xf[:, :, 0:4], 0.0), [], ["xo%d" % t for t in range(NT)])
+    V(128, lambda q: q.tensor_scalar(T.id3[:, :, :], T.row3[:, :, :], own, None, A.is_equal), ["row3", "pf"], ["id3"])
+    select(0)
+    V(128, lambda q: q.tensor_scalar(eye[:, 0:128], T.row[:, 15:143], own, None, A.is_equal), ["row", "pf"], ["eye"])
+    V(144, lambda q: q.tensor_scalar(T.ee[:, :], T.row[:, :], grp, None, A.is_equal), ["row", "pf"], ["ee"])
+    S(128, lambda q: q.activation(neg, eye, AF.Copy, scale=-1.0), ["eye"], ["neg"])
+    S(144, lambda q: q.activation(T.eh[:, :], T.ee[:, :], AF.Copy, scale=0.5), ["ee"], ["eh"])
+    for j in (1, 2, 3):
+        V(1, lambda q, j=j: q.memset(T.cst[:, j:j + 1], float(j * SL // 4)), [], ["cst%d" % j])
+        S(SL // 4, lambda q, j=j: q.activation(T.big[:, j * SL // 4:(j + 1) * SL // 4], T.big[:, 0:SL // 4], AF.Identity, bias=T.cst[:, j:j + 1]), ["big0", "cst%d" % j], ["big%d" % j])
+    V(16, lambda q: q.tensor_scalar(T.m16[:, :], T.row[:, 15:31], low, None, A.is_equal), ["row", "pf"], ["m16"])
+    V(16, lambda q: q.memset(T.p2[:, 32:48], 2.0), [], ["two"])
+    V(16, lambda q: q.memset(T.p2[:, 48:64], 0.5), [], ["half"])
+    V(32, lambda q: q.memset(T.p2[:, 0:32], 0.0), [], ["p2a", "p2b"])
+    V(16, lambda q: q.memset(T.pm[:, 0:16], 0.0), [], ["pm0"])
+    for t in range(NT):
+        (k, n, a, st), = runs([e[0] for e in plans[t][2]])
+        V(3, lambda q, t=t, a=a, st=st: q.tensor_reduce(T.ind[:, t:t + 1], T.m16[:, a:a + 2 * st + 1:st], AxisListType.X, A.add), ["m16"], ["ind%d" % t])
+    V(M, lambda q: q.tensor_tensor_scan(T.p2[:, 0:M], T.p2[:, 32:32 + M], T.pm[:, 0:M], 0.25, A.mult, A.add), ["two", "pm0"], ["p2a"])
+    V(M, lambda q: q.tensor_tensor_scan(T.p2[:, 16:16 + M], T.p2[:, 48:48 + M], T.pm[:, 0:M], 4.0, A.mult, A.add), ["half", "pm0"], ["p2b"])
+    V(4, lambda q: q.tensor_copy(T.ofs32[:, :], T.ofi[:, :]), ["ofi"], ["ofs32"])
+    first(0)
+    indk = ["ind%d" % t for t in range(NT)]
+    V(4, lambda q: q.tensor_scalar(T.ba[:, :], T.ind[:, :], 8.0, -7.5, A.mult, A.add), indk, ["ba"])
+    V(1, lambda q: q.memset(T.p2[:, M:M + 1], -1024.0), ["p2a"], ["p2c"])
+    V(1, lambda q: q.memset(T.p2[:, M + 1:M + 2], 0.5), ["p2a"], ["p2d"])
+    V(4, lambda q: q.tensor_scalar(T.bs[:, :], T.ind[:, :], 8.0, -8.5, A.mult, A.add), indk, ["bs"])
+    for j in range(2):
+        V(32, lambda q, j=j: q.tensor_tensor(T.pm[:, 16 * j:16 * j + 16], T.p2[:, 16 * j:16 * j + 16], T.m16[:, :], A.mult),
+          ["p2a", "p2b", "p2c", "p2d", "m16"], ["pm%d" % j])
+    V(6, lambda q: q.tensor_tensor(T.ob[:, 0:3], T.ofs32[:, 1:4], T.fi[:, 36:39], A.add), ["ofs32", "fk"], ["ob0"])
+    now[0] = -1
+    for j in range(2):
+        V(16, lambda q, j=j: q.tensor_reduce(T.pc[:, j:j + 1], T.pm[:, 16 * j:16 * j + 16], AxisListType.X, A.add), ["pm%d" % j], ["pc%d" % j])
     V(128, lambda q: q.tensor_scalar(T.gm[0:8, :], T.gi[0:8, :], 0.0, None, A.is_equal), ["gi"], ["gm"])
-    V(4, lambda q: q.tensor_copy(T.thb[0:8, 0:4], T.thi[0:8, :]), ["thi"], ["thb"])
-    op("P", "mm", [4], lambda q: q.matmul(T.zp1[:, 0:4], T.gm[0:8, :], T.thb[0:8, 0:4], True, True), ["gm", "thb"], ["zp1"])
-    V(4, lambda q: q.tensor_copy(T.thf[:, :], T.zp1[:, 0:4]), ["zp1"], ["thf"])
+    V(144, lambda q: q.tensor_scalar(T.ew[:, :], T.ee[:, :], T.pc[:, 0:1], None, A.mult), ["ee", "pc0"], ["ew"])
+    for c in range(1, nc):
+        now[0] = c - 1
+        first(c, "x1")
+    now[0] = -1
+    V(4, lambda q: q.tensor_copy(T.thb[0:8, 0:4], T.thi[0:8, :]), ["thi"], ["thb"], "ub")
+    PE([4], lambda q: q.matmul(T.zp1[:, 0, 0:4], T.gm[0:8, :], T.thb[0:8, 0:4], True, True), ["gm", "thb"], ["zp1"], "sm")
+    V(200, lambda q: q.memset(T.w1[:, :, 0:Z + K], 0.0), [], ["spare%d" % t for t in range(5)], "xf")
+    V(36, lambda q: q.tensor_scalar(T.ff[:, :], T.fi[:, 0:36], low, None, A.add), ["fi", "fj", "pf"], ["ff"], "xf")
+    V(4, lambda q: q.tensor_copy(T.thf[:, :], T.zp1[:, 0, 0:4]), ["zp1"], ["thf"], "xf")
+    V(408, lambda q: q.memset(T.sv[:, 17:68, :], 0.0), [], ["selv1"], "sc")
+    V(840, lambda q: q.memset(T.sc[:, 70:280, :], 0.0), [], ["selc1"], "sc")
+    V(256, lambda q: q.tensor_scalar(T.kc[:, :], T.ki[:, :], low, None, A.is_equal), ["ki", "pf"], ["kc"], "mg")
+    for t in (1, 2, 3):
+        now[0] = prm["SEL"][t - 1]
+        select(t)
+        S(8, lambda q, t=t: q.activation(T.xf[:, nc * t:nc * t + nc, 0:4], T.xf[:, 0:nc, 0:4], AF.Identity, bias=T.ob[:, t - 1:t]), ["xo0", "ob0"], ["xo%d" % t])
 
+    def again(a, b, at):
+        op("G", "g", b - a, lambda q: q.affine_select(T.pw[:, at:at + b - a], T.pw[:, LO + a:LO + b], [[0, b - a]], A.is_ge, 0.0, 0, 0), ["pw"], ["pw%d" % at])
+        wide[1].append("pw%d" % at)
+
+    D, gp = 256, prm["GP"]
+    wide = {0: ["pw"], 1: ["pw", "rep0", "rep3"]}
+    again(0, 512, LO + P)
     send("in0", row * C // 2, 1, slot[0], slot[4], ["slot4"], ["slot0"])
+    again(512, 1024, LO + P + 512)
     send("ex0A", row * C // 2, 1, T.w20[:, 0:C // 2], T.w23[:, 0:C // 2], ["ex3A"], ["ex0A"])
+    again(1024, 1536, LO + P + 1024)
     send("ex0B", row * C // 2, 1, T.w20[:, C // 2:C], T.w23[:, C // 2:C], ["ex3B"], ["ex0B"])
-    dma("rep1", 128 * P * 2, T.pw[:, LO + P:LO + 2 * P], T.pic[:, :], [prm["REP"]], ["pw1"])
-    dma("rep0", 128 * LO * 2, T.pw[:, 0:LO], T.pic[:, P - LO:P], [], ["pw0"])
-    dma("rep2", 128 * LO * 2, T.pw[:, LO + 2 * P:PW], T.pic[:, 0:LO], [], ["pw2"])
+    again(1536, gp, LO + P + 1536)
+    send("in1", row * C // 2, 1, slot[1], slot[0], ["slot0"], ["slot1"])
+    send("ex1", row * C, 2, T.w21[:, 0:C], T.w23[:, 0:C], ["ex3A", "ex3B"], ["ex1A", "ex1B"])
+    again(gp, P, LO + P + gp)
+    dma("rep0", 128 * D * 2, T.pw[:, LO - D:LO], T.pic[:, P - D:P], [], ["rep0"])
+    dma("rep3", 128 * D * 2, T.pw[:, LO + 2 * P:LO + 2 * P + D], T.pic[:, 0:D], [], ["rep3"])
+    dma("rep1", 128 * (LO - D) * 2, T.pw[:, 0:LO - D], T.pic[:, P - LO:P - D], ["@ex1"], ["rep1"])
+    dma("rep2", 128 * (LO - D) * 2, T.pw[:, LO + 2 * P + D:PW], T.pic[:, D:LO], [], ["rep2"])
+    wide[2] = wide[3] = wide[1] + ["rep1", "rep2"]
 
-    def probes(t, f0, f1):
-        x = min(max(prm["MOD"][t], f0), f1)
-        if x > f0:
-            s, n = w2[t][:, C + f0:C + x], x - f0
-            V(n, lambda q: q.tensor_scalar(T.xi[:, f0:x], s, T.off32[:, t:t + 1], None, A.add), keys("s%d" % t, f0, x) + ["off32"], keys("xi", f0, x))
-            V(n, lambda q: q.tensor_scalar(T.xj[:, f0:x], T.xi[:, f0:x], P - 1, None, A.bitwise_and), keys("xi", f0, x), keys("xj", f0, x))
-            V(n, lambda q: q.tensor_copy(T.off[:, f0:x], T.xj[:, f0:x]), keys("xj", f0, x), keys("off", f0, x))
-        if f1 > x:
-            V(f1 - x, lambda q: q.tensor_scalar(T.off[:, x:f1], w2[t][:, C + x:C + f1], T.off32[:, t:t + 1], float(LO), A.add, A.add),
-              keys("s%d" % t, x, f1) + ["off32"], keys("off", x, f1))
+    def lists(t, k, f0, f1):
+        H = f1 - f0
+
+        def fn(q, j, per, out):
+            sel, b = (T.sv, 17 * t + 1) if j == 0 else (T.sc, 35 * (2 * t + j - 1) + 3)
+            for h in range(per):
+                ins = q.matmul(out, sel[:, b - h:b - h + 8 * per, :], T.xf[:, k, 4 - per + h:4 + H:per], h == 0, h == per - 1)
+            return ins
+        for j, per, ps, c0, dst, bank, sk in ((0, 2, T.lv, 0, T.ov[:, f0 // 2:f1 // 2], "lv", selk[t][0] + selk[t][1]),
+                                              (1, 4, T.lc, 0, T.oc[:, f0 // 2:f0 // 2 + H // 4], "lc", selk[t][2]),
+                                              (2, 4, T.lv, 256, T.oc[:, f0 // 2 + H // 4:f1 // 2], "lv", selk[t][3])):
+            n, x = H // per, "vlr"[j]
+            PE([n + 1] * per, lambda q, j=j, per=per, out=ps[:, c0:c0 + n + 1]: fn(q, j, per, out), sk + ["xf%d" % k, "xo%d" % t], [bank], "l" + x, 4)
+            V(n, lambda q, dst=dst, src=ps[:, c0 + 1:c0 + n + 1], ofs=ps[:, c0:c0 + 1]: q.tensor_scalar(dst, src, ofs, None, A.add), [bank], keys("o" + x, f0, f1), ("ov", "ol", "Or")[j])
 
     def patch(t):
-        V(4, lambda q: q.tensor_scalar(T.tl[:, :], mi[t][:, K:K + 4], float(-base[t - 1]), None, A.add), ["mi%d" % t], ["tl"])
-        V(K, lambda q: q.tensor_copy(T.w1[:, base[t]:base[t] + SL].indirect(T.tl[:, :]), mi[t][:, 0:K]),
-          ["tl", "mi%d" % t, "mh%d" % t], ["slot%d" % t, "spare%d" % t], "sca")
+        V(4, lambda q: q.tensor_scalar(T.tl[:, :], mi[t][:, K:K + 4], -X0, None, A.add), ["mi%d" % t], ["tl"], "tl")
+        V(K, lambda q: q.tensor_copy(T.w1[:, t, :].indirect(T.tl[:, :]), mi[t][:, 0:K]),
+          ["tl", "mi%d" % t, "mh%d" % t], ["slot%d" % t, "spare%d" % t], "sca", "sca")
+        if t == 3:
+            V(K, lambda q: q.tensor_copy(T.w1[:, 4, :].indirect(T.tl[:, :]), mi[t][:, 0:K]), ["tl", "mi3", "mh3"], ["slot4", "spare4"], "sc4", "sca")
 
-    def gather(t, a):
-        mod = a < prm["MOD"][t]
-        src = (T.pw[:, LO:LO + P] if mod else T.pw[:, :]).indirect(T.off[:, a:a + 64])
-        r = (["pw"] if mod else ["pw", "pw0", "pw1", "pw2"]) + keys("off", a, a + 64)
-        out = T.u[:, 16 * a:16 * a + 1024]
-        if prm["GE"][t][a // 64] == "V":
-            op("V", "gat", 1024, lambda q: q.tensor_copy(out, src), r, ["u%d" % a])
-        else:
-            op("S", "gat", 1024, lambda q: q.activation(out, src, AF.Copy), r, ["u%d" % a])
+    def piece(t, f0, f1, a, b, j, bank, c0, x):
+        n, q4 = b - a, (f1 - f0) // 4
+        win, wk = T.pw[:, LO - D * t:LO + D * t + (2 * P if t else P)], wide[t]
+        left, right, pairs = plans[t]
+        uk = keys("u", a, b)
+        S(8 * n, lambda q: q.activation(T.u[:, 8 * a:8 * b], win.indirect(T.ov[:, a // 2:b // 2]), AF.Copy), wk + keys("ov", a, b), uk, "u" + x, "gat")
+        for out, name, l0, w, cmp in ((T.cl, "cl", 0, 0, A.is_gt), (T.cr, "cr", q4, RIGHT[t], A.is_lt)):
+            c1 = f0 // 2 + l0 + (a - f0) // 4
+            V(4 * n, lambda q, out=out, c1=c1, w=w, cmp=cmp: q.tensor_tensor(out[:, 4 * a:4 * b], win.indirect(T.oc[:, c1:c1 + n // 4]), T.u[:, 8 * a + w:8 * b:2], cmp),
+              wk + keys("o" + name[1], f0, f1) + uk, keys(name, a, b), name + x, "gat")
 
-    def compare(t, a, j):
-        d, eng = 5 - t, prm["CE"][t][a // 64]
-        for h, (m0, m1) in enumerate(((0, 8), (8, M))):
-            ps, out, pk = cp[j][:, 64 * h:64 * h + 64, 0:m1 - m0], T.cmp[:, a:a + 64, m0:m1], "cp%d%d" % (j, h)
+        def diffs(q):
+            for e, (m, z, y) in enumerate(pairs):
+                q.matmul(dp[j][:, e, 0:n], eye, T.u[:, 8 * a + z:8 * b:8], True, False)
+                ins = q.matmul(dp[j][:, e, 0:n], neg, T.u[:, 8 * a + y:8 * b:8], False, True)
+            return ins
+        PE([n] * 6, diffs, ["eye", "neg"] + uk, ["dp%d" % j], "df" + x)
+        S(3 * n, lambda q: q.activation(T.sg[:, :, a:b], dp[j][:, 0:3, 0:n], AF.Sign, bias=T.cst[:, 0:1]), ["dp%d" % j, "tiny"], keys("sg", a, b), "sg" + x)
+        terms = [(T.eh, m, T.sg[:, e, a:b]) for e, (m, z, y) in enumerate(pairs)]
+        terms += [(T.ee, m, T.cl[:, 4 * a + k:4 * b:4]) for k, m in enumerate(left)]
+        terms += [(T.ee, m, T.cr[:, 4 * a + k:4 * b:4]) for k, m in enumerate(ROWS[t][RIGHT[t]])]
 
-            def fill(q, h=h, m0=m0, m1=m1):
-                for m in range(m0, m1):
-                    o = cp[j][:, 64 * h:64 * h + 64, m - m0]
-                    q.matmul(o, eye[0], T.u[:, 16 * a + m:16 * a + 1024:16], True, False)
-                    ins = q.matmul(o, eye[M], T.u[:, 16 * a + m + d:16 * a + 1024:16], False, True)
-                return ins
-            n = 64 * (m1 - m0)
-            op("P", "mm", [n, n], fill, ["id0", "id%d" % M, "u%d" % a], [pk])
-            ck = ["cmp%d_%d" % (a // 64, h)]
-            if eng == "S":
-                op("S", "c", n, lambda q, ps=ps, out=out: q.activation(out, ps, AF.Sign, bias=T.cst[:, 0:1]), [pk, "tiny"], ck)
-            else:
-                V(n, lambda q, ps=ps, out=out: q.tensor_scalar(out, ps, 0.0, None, A.is_gt), [pk], ck)
+        def votes(q):
+            for i, (wt, m, rhs) in enumerate(terms):
+                ins = q.matmul(vp[bank][:, a - c0:b - c0], wt[:, 15 - m:143 - m], rhs, i == 0, i == M - 1)
+            return ins
+        PE([n] * M, votes, ["ee", "eh"] + keys("sg", a, b) + keys("cl", a, b) + keys("cr", a, b), ["vp%d" % bank], "vt" + x)
 
-    def votes(t, c, f0, x, y):
-        sign = prm["CE"][t][x // 64] == "S"
-        out = vp[c][:, (x - f0) // 16:(y - f0) // 16, 0:M]
+    def marks(t, a, b, bank, x):
+        n, vk, cnt = b - a, "vp%d" % bank, vp[bank][:, 0:b - a]
+        S(n, lambda q: q.activation(T.ab[:, a:b], cnt, AF.Abs, bias=T.ba[:, t:t + 1]), [vk, "ba"], keys("ab", a, b), "ab" + x)
+        S(n, lambda q: q.activation(T.ft[:, 0, a:b], cnt, AF.Sign, bias=T.bs[:, t:t + 1]), [vk, "bs"], keys("fb", a, b), "fb" + x)
+        V(n // 2, lambda q: q.tensor_scalar(T.ft[:, 1, a:b], T.ab[:, a:b], 4.0, T.pc[:, 1:2], A.is_ge, A.mult), keys("ab", a, b) + ["pc1"], keys("fe", a, b), "fe" + x)
 
-        def fn(q):
-            if sign:
-                q.matmul(out, eye[3], T.one[:, 0:(y - x) // 16, :], True, False)
+    def tail(t, k, f0, f1, nys):
+        c = k % 2
+        n, na, a0, a1, zk = f1 - f0, (f1 - f0) // 16, f0 // 16, f1 // 16, "zp%d" % c
+
+        def sums(q):
             for b in range(16):
-                ins = q.matmul(out, (T.eh if sign else T.ee)[:, 15 - b:143 - b], T.cmp[:, x + b:y:16, :], b == 0 and not sign, b == 15)
+                ins = q.matmul(zp[c][:, :, 0:na], T.ew[:, 15 - b:143 - b], T.ft[:, :, f0 + b:f1:16], b == 0, b == 15)
             return ins
-        op("P", "mm", [(y - x) // 16 * M] * (17 if sign else 16), fn,
-           ["ee", "eh", "one", "id3"] + ["cmp%d_%d" % (z, h) for z in range(x // 64, y // 64) for h in (0, 1)], ["vp%d" % c])
-
-    def tail(t, c, f0, f1, nys):
-        n, na, a0 = f1 - f0, (f1 - f0) // 16, f0 // 16
-        vk, fk, cnt = "vp%d" % c, ["ft%d%d" % (c, j) for j in range(3)], vp[c][:, 0:na, 0:M]
-        fs = [ft[c][:, 16 * j:16 * j + na, :] for j in range(3)]
-        op("S", "c", na * M, lambda q: q.activation(fs[0], cnt, AF.Abs, bias=T.cst[:, 4:5]), ["mid"], [fk[0], vk])
-        V(na * M, lambda q: q.tensor_scalar(fs[2], cnt, 9.0, None, A.is_ge), [vk], [fk[2]])
-        V(na * M // 2, lambda q: q.tensor_scalar(fs[1], fs[0], 4.0, None, A.is_ge), [fk[0]], [fk[1]])
-
-        def sums(q, j):
-            for m in range(M):
-                if j == 1:
-                    ins = q.matmul(zp[c][:, 0:na], eye[0], ft[c][:, 16:16 + na, m], m == 0, m == M - 1)
-                else:
-                    ins = q.matmul(zp[c][:, 16:16 + na], eye[m], ft[c][:, 32:32 + na, m], m == 0, m == M - 1)
-            return ins
-        for j in (2, 1):
-            op("P", "mm", [na] * M, lambda q, j=j: sums(q, j), [fk[j]] + idk, ["zp%d" % c])
-        ub, t2, t3 = T.ub[:, a0:a0 + na], T.tb[:, 2 * a0:2 * a0 + na], T.tb[:, 2 * a0 + na:2 * a0 + 2 * na]
-        kub, kt, ku, kil, kup = keys("ub", f0, f1), keys("ta", f0, f1), keys("tb", f0, f1), keys("il", f0, f1), keys("up", f0, f1)
-        V(na, lambda q: q.tensor_scalar(ub, zp[c][:, 0:na], T.thf[:, t:t + 1], float(base[t] + K), A.is_ge, A.mult), ["zp%d" % c, "thf"], kub)
-        V(na, lambda q: q.tensor_tensor(t2, zp[c][:, 16:16 + na], ub, A.add), ["zp%d" % c] + kub, kt + ku)
-        V(2 * na, lambda q: q.tensor_tensor(t3, t2, T.ff[:, a0:a0 + na], A.min), kt + ["ff"], ku)
-        V(2 * na, lambda q: q.tensor_copy(T.il[:, 2 * a0:2 * a0 + 2 * na], T.tb[:, 2 * a0:2 * a0 + 2 * na]), kt + ku, kil)
-        r = ["zero"] + ["slot%d" % j for j in range(t + 1)] + ["spare%d" % j for j in range(1, t + 1)] + kil
-        src = T.w1[:, 0:base[t] + SL].indirect(T.il[:, 2 * a0:2 * a0 + na])
-        if (t, f0) in prm["G1S"]:
-            op("S", "gat", n, lambda q: q.activation(T.up[:, f0:f1], src, AF.Copy), r, kup)
+        PE([2 * na] * 16, sums, ["ew"] + keys("fb", f0, f1) + keys("fe", f0, f1), [zk], "sm")
+        ub, ta, tb = T.ub[:, a0:a1], T.ta[:, a0:a1], T.tb[:, a0:a1]
+        kub, kta, ktb, kia, kib, kup = (keys(x, f0, f1) for x in ("ub", "ta", "tb", "ia", "ib", "up"))
+        V(na, lambda q: q.tensor_scalar(ub, zp[c][:, 1, 0:na], T.thf[:, t:t + 1], SURE, A.is_ge, A.mult), [zk, "thf"], kub, "ub")
+        V(na, lambda q: q.tensor_tensor(ta, zp[c][:, 0, 0:na], ub, A.add), [zk] + kub, kta, "ta")
+        V(na, lambda q: q.tensor_scalar(T.ia[:, a0:a1], ta, -X0, None, A.add), kta, kia, "ia")
+        V(2 * na, lambda q: q.tensor_tensor(tb, ta, T.ff[:, a0:a1], A.min), kta + ["ff"], ktb, "tb")
+        V(na, lambda q: q.tensor_copy(T.ib[:, a0:a1], tb), ktb, kib, "ib")
+        S(n, lambda q: q.activation(T.up[:, f0:f1], T.w1[:, t, :].indirect(T.ia[:, a0:a1]), AF.Copy),
+          ["slot%d" % t, "spare%d" % t] + kia, kup, "up", "gat")
+        new, nk = (T.xf[:, k + nc, 4:4 + n], ["xf%d" % (k + nc)]) if t < 3 else (T.xi[:, f0:f1], keys("xi", f0, f1))
+        V(n, lambda q: q.tensor_tensor(new, w2[t][:, 0:C + f1].indirect(T.ib[:, a0:a1]), T.up[:, f0:f1], A.add),
+          ["ex%dA" % t, "ex%dB" % t] + keys("s%d" % t, 0, f1) + kib + kup, nk, "xf", "gat")
+        if t < 3 and prm["SC"] == "G":
+            op("G", "g", n, lambda q: q.affine_select(w2[t + 1][:, C + f0:C + f1], new, [[0, n]], A.is_ge, 0.0, 0, 0), nk, keys("s%d" % (t + 1), f0, f1))
+        elif t < 3:
+            V(n, lambda q: q.tensor_copy(w2[t + 1][:, C + f0:C + f1], new), nk, keys("s%d" % (t + 1), f0, f1), "sc")
         else:
-            op("V", "gat", n, lambda q: q.tensor_copy(T.up[:, f0:f1], src), r, kup)
-        new, nk = (w2[t + 1][:, C + f0:C + f1], keys("s%d" % (t + 1), f0, f1)) if t < 3 else (T.xi[:, f0:f1], keys("xi", f0, f1))
-        op("V", "gat", n, lambda q: q.tensor_tensor(new, w2[t][:, :].indirect(T.il[:, 2 * a0 + na:2 * a0 + 2 * na]), T.up[:, f0:f1], A.add),
-           ["ex%dA" % t, "ex%dB" % t] + keys("s%d" % t, 0, F) + kil + kup, nk)
-        if t < 3:
-            probes(t + 1, f0, f1)
-        else:
-            V(n, lambda q: q.tensor_scalar(T.xj[:, f0:f1], T.xi[:, f0:f1], P - 1, None, A.bitwise_and), nk, keys("xj", f0, f1))
-            V(n, lambda q: q.tensor_copy(T.yf[:, f0:f1], T.xj[:, f0:f1]), keys("xj", f0, f1), keys("yf", f0, f1))
-            dma("ys%d" % nys, row * n, T.ys[:, f0:f1], T.yf[:, f0:f1], keys("yf", f0, f1), [], "S" if nys else "Y")
+            V(n, lambda q: q.tensor_scalar(T.xj[:, f0:f1], T.xi[:, f0:f1], P - 1, None, A.bitwise_and), nk, keys("xj", f0, f1), "And")
+            V(n, lambda q: q.tensor_copy(T.yf[:, f0:f1], T.xj[:, f0:f1]), keys("xj", f0, f1), keys("yf", f0, f1), "yf")
+            dma("ys%d" % nys, row * n, T.ys[:, f0:f1], T.yf[:, f0:f1], keys("yf", f0, f1), [])
         if f0 <= K * t < f1:
-            halve(t, T.tb[:, a0 + 4 * t:a0 + 4 * t + 4], kt, kup)
+            halve(t, kta + kia, kup)
 
-    def halve(t, t2, kt, kup):
-        spare = T.ff[:, 32 + 4 * t:36 + 4 * t]
+    def halve(t, kt, kup):
+        spare = T.ff[:, 32:36]
         mk, hk = ("mo%d" % t, "mg%d" % t) if t < 3 else ("mi4", "mh4")
-        V(8, lambda q: q.tensor_tensor(T.y0[:, :], t2, spare, A.max), kt + ["ff"], ["y0"])
-        V(4, lambda q: q.tensor_scalar(T.yl[:, :], T.y0[:, :], float(-base[t]), None, A.add), ["y0"], ["yl"])
+        bk = ["big%d" % j for j in range(4)]
         for a in range(4):
-            op("V", "gat", K, lambda q, a=a: q.tensor_scalar(T.ne[:, K * a:K * a + K], T.big[:, :].indirect(T.yl[:, :]), float(base[t]), T.y0[:, a:a + 1], A.add, A.not_equal),
-               ["big", "yl", "y0"], ["ne%d" % a])
-        V(128, lambda q: q.tensor_tensor_scan(T.kp[:, :], T.ne[:, :], T.kc[:, :], 0.0, A.mult, A.max), ["ne0", "ne1", "ne2", "ne3", "kc"], ["kp"])
-        V(8, lambda q: q.tensor_tensor(T.ym[:, :], T.kp[:, K - 1::K], T.y0[:, :], A.mult), ["kp", "y0"], ["ym"])
-        V(8, lambda q: q.tensor_tensor(mo[t][:, K:K + 4], T.ym[:, :], spare, A.max), ["ym", "ff"], [mk])
-        V(K, lambda q: q.tensor_scalar(mo[t][:, 0:K], T.up[:, K * t:K * t + K], 0.5, -0.25, A.mult, A.add), kup, [hk])
+            out, src, mine = T.ne[:, K * a:K * a + K], T.big[:, :].indirect(T.ia[:, 4 * t:4 * t + 4]), T.ta[:, 4 * t + a:4 * t + a + 1]
+            if prm["NE"][a] == "V":
+                V(K, lambda q, out=out, src=src, mine=mine: q.tensor_scalar(out, src, mine, None, A.not_equal), bk + kt, ["ne%d" % a], "ne", "gat")
+            else:
+                S(K, lambda q, out=out, src=src, mine=mine: q.activation(out, src, AF.Abs, bias=mine, scale=-1.0), bk + kt, ["ne%d" % a], "ne", "gat")
+        V(128, lambda q: q.tensor_tensor_scan(T.kp[:, :], T.ne[:, :], T.kc[:, :], 0.0, A.min, A.max), ["ne0", "ne1", "ne2", "ne3", "kc"], ["kp"], "kp")
+        V(8, lambda q: q.tensor_tensor(T.ym[:, :], T.kp[:, K - 1::K], T.ta[:, 4 * t:4 * t + 4], A.mult), ["kp"] + kt, ["ym"], "ym")
+        V(8, lambda q: q.tensor_tensor(mo[t][:, K:K + 4], T.ym[:, :], spare, A.max), ["ym", "ff"], [mk], "mo")
+        V(K, lambda q: q.tensor_scalar(mo[t][:, 0:K], T.up[:, K * t:K * t + K], 0.5, -0.25, A.mult, A.add), kup, [hk], "mg")
         if t < 3:
             send("m%d" % (t + 1), row * 68, 1, mi[t + 1][:, :], mo[t][:, :], [mk, hk], ["mi%d" % (t + 1), "mh%d" % (t + 1)])
         else:
+            k, now[0] = now[0], 4 * nc
             patch(4)
+            now[0] = k
             dma("yi", row * C // 2, T.yi[:, :], slot[4], ["slot4"], [])
 
-    probes(0, 0, H)
-    probes(0, H, F)
-    ncp, nch = 0, 0
     for t in range(NT):
+        now[0] = nc * t
+        if t == 3:
+            dma("cp4", row * C // 2, slot[4], slot[3], ["slot3"], ["slot4"])
         if t > 0:
             patch(t)
-        if t < 3:
+        if t in (1, 2):
             send("in%d" % (t + 1), row * C // 2, 1, slot[t + 1], slot[t], ["slot%d" % t], ["slot%d" % (t + 1)])
-        else:
-            dma("cp4", row * C // 2, slot[4], slot[3], ["slot3"], ["slot4"])
-        if t < 2:
-            send("ex%d" % (t + 1), row * C, t + 2, w2[t + 1][:, 0:C], T.w23[:, 0:C], ["ex3A", "ex3B", "slot%d" % t], ["ex%dA" % (t + 1), "ex%dB" % (t + 1)])
-        ch = prm["CH"][t]
-        for nys, (f0, f1) in enumerate(zip(ch[:-1], ch[1:])):
-            for a in range(f0, f1, 64):
-                gather(t, a)
-            for a in range(f0, f1, 64):
-                compare(t, a, ncp % 2)
-                ncp += 1
-                if a % 128:
-                    votes(t, nch % 2, f0, a - 64, a + 64)
-            tail(t, nch % 2, f0, f1, nys)
-            nch += 1
+        if t == 1:
+            send("ex2", row * C, 3, T.w22[:, 0:C], T.w23[:, 0:C], ["ex3A", "ex3B"], ["ex2A", "ex2B"])
+        for c, cut in enumerate(ch):
+            now[0] = k = nc * t + c
+            f0, f1, last = cut[0], cut[-1], cut[-2] if prm["FS"] else -1
+            lists(t, k, f0, f1)
+            for x, (a, b) in enumerate(zip(cut[:-1], cut[1:])):
+                bank = int(a == last) if prm["FS"] else k % 2
+                piece(t, f0, f1, a, b, count[0] % 2, bank, a if a == last else f0, str(x + 5 - len(cut)))
+                count[0] += 1
+                if b in (last, f1):
+                    marks(t, a if a == last else f0, b, bank, str(int(b == f1)))
+            tail(t, k, f0, f1, c)
     return ops
 
 
 def link(ops):
-    last, readers, sends = {}, {}, {}
+    last, readers = {}, {}
+    sends = {o["name"]: i for i, o in enumerate(ops) if o["kind"] == "rem"}
     for i, o in enumerate(ops):
         deps = set()
-        if o["kind"] == "rem":
-            sends[o["name"]] = i
         if o["kind"] == "arr":
             o["src"] = sends[o["name"]]
         for key in o["r"]:
@@ -287,6 +393,8 @@ def link(ops):
                 deps.add(sends[key[1:]])
             elif key in last:
                 deps.add(last[key])
+            if key in BANKS:
+                deps.update(j for j in readers.get(key, []) if ops[j]["eng"] != o["eng"])
         if o["kind"] != "arr":
             for key in o["w"]:
                 if key in last:
@@ -301,14 +409,59 @@ def link(ops):
         o["deps"] = sorted(deps)
 
 
+def span(o):
+    n, cyc = o["n"], 0.87e-3
+    if o["kind"] == "mm":
+        return sum(max(64, x) for x in n) * o["w4"] * cyc / 2
+    if o["kind"] in ("gat", "sca"):
+        return 0.055 + n * cyc * (1.5 if o["kind"] == "gat" else 3.5)
+    if o["kind"] == "g":
+        return 0.15 + 2 * n * cyc
+    return {"dma": 0.1, "rem": 0.3}.get(o["kind"], max(64, n) * cyc)
+
+
+def schedule(ops, lag, wake=0.2, wait=0.05, fly=1.7, rate=450e3):
+    rank = [o["chunk"] + lag.get(o["tag"], 1) + i * 1e-6 for i, o in enumerate(ops)]
+    left, ready, users = [len(o["deps"]) for o in ops], [0.0] * len(ops), [[] for o in ops]
+    for i, o in enumerate(ops):
+        for j in o["deps"]:
+            users[j].append(i)
+    arr = {o["src"]: i for i, o in enumerate(ops) if o["kind"] == "arr"}
+    todo = {e: [i for i, o in enumerate(ops) if o["eng"] == e] for e in "VSPGY"}
+    pool = {e: [i for i in todo[e] if not left[i]] for e in "VSP"}
+    order, free, pipe = {e: [] for e in todo}, {e: 0.0 for e in todo}, 0.0
+
+    def done(i, t):
+        for j in users[i]:
+            ready[j] = max(ready[j], t if ops[i]["eng"] == "P" == ops[j]["eng"] else t + wake)
+            left[j] -= 1
+            if not left[j] and ops[j]["eng"] in pool:
+                pool[ops[j]["eng"]].append(j)
+    for step in range(sum(len(v) for v in todo.values())):
+        for e in "GY":
+            pool[e] = [i for i in todo[e][len(order[e]):len(order[e]) + 1] if not left[i]]
+        at, e = min((max(free[e], min(ready[i] for i in pool[e])), e) for e in pool if pool[e])
+        i = min((j for j in pool[e] if ready[j] <= at + wait), key=lambda j: rank[j])
+        pool[e].remove(i)
+        order[e].append(i)
+        free[e] = max(free[e], ready[i]) + span(ops[i])
+        if ops[i]["kind"] in ("dma", "rem"):
+            pipe = max(pipe, free[e] + 0.6 * fly) + ops[i]["n"] / rate
+            for j in (i, arr.get(i)):
+                if j is not None:
+                    done(j, pipe + 0.4 * fly)
+        else:
+            done(i, free[e])
+    return order
+
+
 def rank_program(g, core, T, topo):
     rank = T.rank_of(core)
     if rank is None:
         return
     ops = build(T, topo, core, rank, PRM)
     link(ops)
-    order = {e: [i for i, o in enumerate(ops) if o["eng"] == e] for e in "GY"}
-    order.update(ORDERS)
+    order = schedule(ops, PRM["LAG"])
     queue = {"V": g.vector, "S": g.scalar, "P": g.tensor, "G": g, "Y": g.sync}
     needed = set()
     for o in ops:

@@ -6,8 +6,9 @@ LO = 768
 PW = LO + 2 * P + LO
 Z = 16
 SL = Z + K + C
-SURE = 4096.0
-X0 = SURE - Z - K
+E = Z + K
+SURE, FAR = 4096.0, 1e6
+WS = C + F
 TINY = 2.0 ** -108
 BF, F32, I32, U16 = "bfloat16", "float32", "int32", "uint16"
 
@@ -17,13 +18,12 @@ RIGHT = [0, 1, 0, 0]
 SCRATCH = {
     "pw": ("sbuf", [128, PW], BF), "u": ("sbuf", [128, F * 8], BF), "cl": ("sbuf", [128, F * 4], BF), "cr": ("sbuf", [128, F * 4], BF),
     "sg": ("sbuf", [128, 3, F], BF), "w1": ("sbuf", [128, 5, SL], BF),
-    "w20": ("sbuf", [128, C + F], I32), "w21": ("sbuf", [128, C + F], I32),
-    "w22": ("sbuf", [128, C + F], I32), "w23": ("sbuf", [128, C + F], I32),
-    "xi": ("sbuf", [128, F], I32), "xj": ("sbuf", [128, F], I32), "xf": ("sbuf", [128, 4 * NT, H + 4], F32), "yf": ("sbuf", [128, F], F32),
-    "ov": ("sbuf", [128, F // 2], U16), "oc": ("sbuf", [128, F // 2], U16), "up": ("sbuf", [128, F], F32),
-    "ab": ("sbuf", [128, F], BF), "ft": ("sbuf", [128, 2, F], BF),
-    "ub": ("sbuf", [128, 32], F32), "ta": ("sbuf", [128, 32], F32), "tb": ("sbuf", [128, 32], F32),
-    "ia": ("sbuf", [128, 32], U16), "ib": ("sbuf", [128, 32], U16),
+    "w2": ("sbuf", [128, E + NT * WS], I32),
+    "xi": ("sbuf", [128, F], I32), "xj": ("sbuf", [128, F], I32), "xf": ("sbuf", [128, NT, F + 4], F32), "yf": ("sbuf", [128, F], F32),
+    "ov": ("sbuf", [128, F // 2], U16), "ol": ("sbuf", [128, F // 4], U16), "oc": ("sbuf", [128, F // 4], U16), "up": ("sbuf", [128, F], F32),
+    "ab": ("sbuf", [128, F], BF), "ft": ("sbuf", [128, F, 2], BF),
+    "ka": ("sbuf", [128, 64], F32), "kb": ("sbuf", [128, 64], F32), "tt": ("sbuf", [128, 128], F32), "il": ("sbuf", [128, 64], U16),
+    "pq": ("sbuf", [128, 4], F32),
     "ofi": ("sbuf", [128, 4], I32), "ofs32": ("sbuf", [128, 4], F32), "ob": ("sbuf", [128, 4], F32), "oh": ("sbuf", [128, 4], F32),
     "thi": ("sbuf", [128, 4], I32), "thb": ("sbuf", [128, 8], BF), "thf": ("sbuf", [128, 4], F32),
     "row": ("sbuf", [128, 144], F32), "row3": ("sbuf", [128, 8, 16], F32), "big": ("sbuf", [128, SL], F32), "cst": ("sbuf", [128, 8], F32),
@@ -42,17 +42,29 @@ SCRATCH = {
     "lv": ("psum", [128, 512], F32), "lc": ("psum", [128, 512], F32),
     "dp0": ("psum", [128, 4, 128], F32), "dp1": ("psum", [128, 4, 128], F32),
     "vp0": ("psum", [128, 512], F32), "vp1": ("psum", [128, 512], F32),
-    "zp0": ("psum", [128, 2, 256], F32), "zp1": ("psum", [128, 2, 256], F32),
+    "zp0": ("psum", [128, 512], F32), "lr": ("psum", [128, 512], F32),
 }
 BANKS = [n for n in SCRATCH if SCRATCH[n][0] == "psum"]
-DMAS = ["shpA", "shpB", "ofs", "thr", "pic", "exA", "exB", "inc", "rep0", "rep3", "rep1", "rep2", "cp4", "yi", "ys0", "ys1", "ys2", "ys3"]
+SEATS = [(0, 192, K), (192, 256, 0), (256, F, 256)]
+DMAS = ["shp0", "shp1", "shp2", "ofs", "thr", "pic", "exA", "exB", "inc", "rep0", "rep3", "rep1", "rep2", "cp4", "yi", "ys0", "ys1", "ys2", "ys3", "ys4"]
 SENDS = ["ex0A", "ex0B", "in0", "ex1", "ex2", "in1", "in2", "in3", "m1", "m2", "m3"]
 SEMAPHORES = ["eV", "eS", "eP", "eG"] + ["d_" + n for n in DMAS] + ["l_" + n for n in SENDS] + ["r_" + n for n in SENDS]
 
-LAG = dict(And=-3.5, KP=-1, MG=-0.5, MO=-6, NE=6, Or=-6, SCA=-5.5, TL=-6, YM=-5, ab1=0, cl2=-3, cl3=1.5, cr2=6, cr3=1, df2=-1, df3=1.5, fb1=0.5,
-           fe1=-0.5, ia=-5, ib=-6, kp=-3.5, ll=-0.5, lr=-2, lv=-4, mg=6, mo=4, ne=6, ol=6, ov=1.5, sc=-1, sc4=-5, sca=0, sg2=-4.5, sg3=-3.5,
-           sm=5, ta=-5.5, tb=-3.5, tl=4.5, u2=1.5, u3=6, ub=-5.5, up=-3.5, vt2=5, vt3=0, x1=0.5, xf=0.5, yf=-2, ym=6)
-PRM = dict(LAG=LAG, SEL=[0, 0, 1], GP=2560, FS=False, NE="SSVV", SC="G", CH=[[0, 96, 192], [192, 272, 352], [352, 432, 512]])
+TURN = {
+    "Sstart": "s1A b1A b2A",
+    "Vstart": "k8A x1A k1A x2A k2A x3A k3A k6A OVA k4A k7A k5A x1B x1C t1A x2B ORA x2C x3B OLA t3A x3C",
+    "Pstart": "LVA LLA LRA t2A LVB",
+    "Sround": "s2A u2A ne1B- ne0B- u3A upC- sg2A u2B sg3A u3B sg2B ab1A fb1A u2C sg3B u3C sg2C ab1B fb1B upA sg3C ne0A ne1A ab1C fb1C upB",
+    "Vround": "mgA- kpA- fe1C- xfB- ymA- olA ne3B- mgB- moA- ne2B- OrA taC- tbC- cl2A kpB- ilC- OVB ovB cr2A ymB- cl3A moB- xfC- OrB cr3A ORB t4A "
+              "olB OLB OVC cr2B cl2B ovC cr3B fe1A OLC ORC cl3B tlA olC OrC scaA cl2C tbA taA cr2C ilA cl3C fe1B cr3C xfA ne2A taB tbB ne3A ilB ovA+",
+    "Pround": "lrA llA smC- lvB df2A LRB llB lrB LLB df3A vt2A LVC lvC df2B vt3A LLC llC lrC LRC df3B smA vt2B df2C vt3B df3C vt2C smB vt3C lvA+",
+    "Send": "u2A u3A sg2A upC- u2B sg3A u3B sg2B ab1A fb1A u2C sg3B u3C ab1B fb1B sg2C sg3C upA ne1A AB1C ne0A FB1C ab1C fb1C upB UPC upC",
+    "Vend": "fe1C- kpA- xfB- mgA- ymA- olA moA- OrA taC- tbC- cl2A ilC- ovB cr2A cl3A xfC- olB cr3A OrB cl2B tlA cr2B ovC cr3B fe1A cl3B olC scaA OrC "
+            "sc4A cl2C taA tbA cr2C ilA cr3C fe1B ne3A cl3C ne2A xfA FE1C kpA AndA ymA taB tbB fe1C moA mgA ilB TLA TAC TBC SCAA ILC taC tbC xfB ilC "
+            "AndB XFC xfC ANDC AndC YFC yfC",
+    "Pend": "llA lrA smC- lvB df2A lrB llB df3A vt2A lvC df2B vt3A lrC llC df3B vt2B smA vt3B df2C df3C vt2C smB vt3C SMC smC",
+}
+PRM = dict(TURN=TURN, JOIN=False, GP=3072, END=448, NE="SSVV", SC="G", CH=[[0, 96, 192], [192, 272, 352], [352, 432, 512]])
 
 
 def keys(name, a, b, step=16):
@@ -85,12 +97,13 @@ def plan(t):
 
 def build(T, topo, core, rank, prm):
     A, AF = AluOpType, ActivationFunctionType
-    ops, now, count, ch = [], [-9], [0], prm["CH"]
-    nc = len(ch)
-    mine = [(4 * nc, "tl"), (4 * nc, "sca")] + [(3 * nc + c, x) for c in range(nc) for x in "ne kp ym mo mg".split()]
+    ops, now, count, ch = [], [-9, None], [0, 0], prm["CH"]
+    nc, early = len(ch), [False]
+    mine = [(c, x) for c in range(nc) for x in "lv ov ll ol lr Or".split()] + [(4 * nc, "tl"), (4 * nc, "sca")]
 
     def op(eng, kind, n, fn, r, w, name=None, tag=None):
-        if (now[0], tag) in mine:
+        tag = tag or now[1]
+        if (now[0], tag) in mine or (tag and early[0]):
             tag = tag.upper()
         ops.append(dict(eng=eng, kind=kind, n=n, fn=fn, r=list(r), w=list(w), name=name, chunk=now[0], tag=tag))
 
@@ -120,8 +133,8 @@ def build(T, topo, core, rank, prm):
         n = pattern[0][1] * (pattern[1][1] if len(pattern) > 1 else 1)
         op("G", "g", n, lambda q: q.iota(out, pattern, base, mult, allow_small_or_imprecise_dtypes=True), [], [key])
 
-    w2 = [T.w20, T.w21, T.w22, T.w23]
-    dp, vp, zp = [T.dp0, T.dp1], [T.vp0, T.vp1], [T.zp0, T.zp1]
+    w2 = [T.w2[:, E + WS * t:E + WS * t + WS] for t in range(NT)]
+    dp, vp, zp = [T.dp0, T.dp1], [T.vp0, T.vp1], [T.zp0, T.lr]
     mo, mi = [T.mo0, T.mo1, T.mo2, T.mo3], [None, T.mi1, T.mi2, T.mi3, T.mo3]
     slot = [T.w1[:, t, Z + K:SL] for t in range(5)]
     row = 128 * 4
@@ -138,34 +151,43 @@ def build(T, topo, core, rank, prm):
                 else:
                     out = T.sc[:, 35 * (2 * t + j - 2) + 3:35 * (2 * t + j - 1):4, k:k + n]
                 src = T.id3[:, :, a:a + st * (n - 1) + 1:st]
-                S(8 * n, lambda q, out=out, src=src: q.activation(out, src, AF.Copy), ["id3", "selv%d" % min(t, 1), "selc%d" % min(t, 1)], ["sel%d_%d_%d" % (t, j, k)])
+                r, w = ["id3", ("selv%d" if j < 2 else "selc%d") % t], ["sel%d_%d_%d" % (t, j, k)]
+                if t < 2:
+                    S(8 * n, lambda q, out=out, src=src: q.activation(out, src, AF.Copy), r, w)
+                else:
+                    op("G", "g", 8 * n, lambda q, out=out, src=src, n=n: q.affine_select(out, src, [[0, 8 * n]], A.is_ge, 0.0, 0, 0), r, w)
 
-    def first(c, tag=None):
+    def clear(t):
+        iota(T.sv[:, 17 * t:17 * t + 17, :], [[0, 136]], 0, 0, "selv%d" % t)
+        iota(T.sc[:, 70 * t:70 * t + 70, :], [[0, 280]], 0, 0, "selc%d" % t)
+
+    def first(c):
         f0, f1 = ch[c][0], ch[c][-1]
         n = f1 - f0
-        V(n, lambda q: q.tensor_scalar(T.xi[:, f0:f1], T.w20[:, C + f0:C + f1], T.ofs32[:, 0:1], None, A.add), keys("s0", f0, f1) + ["ofs32"], keys("xi", f0, f1), tag)
-        V(n, lambda q: q.tensor_scalar(T.xj[:, f0:f1], T.xi[:, f0:f1], P - 1, None, A.bitwise_and), keys("xi", f0, f1), keys("xj", f0, f1), tag)
-        V(n, lambda q: q.tensor_copy(T.xf[:, c, 4:4 + n], T.xj[:, f0:f1]), keys("xj", f0, f1), ["xf%d" % c], tag)
+        V(n, lambda q: q.tensor_scalar(T.xi[:, f0:f1], w2[0][:, C + f0:C + f1], T.ofs32[:, 0:1], None, A.add), keys("s0", f0, f1) + ["ofs32"], keys("xi", f0, f1), "x1")
+        V(n, lambda q: q.tensor_scalar(T.xj[:, f0:f1], T.xi[:, f0:f1], P - 1, None, A.bitwise_and), keys("xi", f0, f1), keys("xj", f0, f1), "x2")
+        V(n, lambda q: q.tensor_copy(T.xf[:, 0, 4 + f0:4 + f1], T.xj[:, f0:f1]), keys("xj", f0, f1), keys("xf0_", f0, f1), "x3")
 
-    H = ch[0][-1]
     dma("ofs", row * 4, T.ofi[:, :], T.ofs[:, :], [], ["ofi"])
-    dma("shpA", row * H, T.w20[:, C:C + H], T.shp[:, 0:H], [], keys("s0", 0, H), "S")
+    dma("shp0", row * 192, w2[0][:, C:C + 192], T.shp[:, K:K + 192], [], keys("s0", 0, 192), "S")
     dma("pic", 128 * P * 2, T.pw[:, LO:LO + P], T.pic[:, :], [], ["pw"])
-    dma("shpB", row * H, T.w20[:, C + H:C + F], T.shp[:, H:F], [], keys("s0", H, F))
+    for j, (a, b, f) in list(enumerate(SEATS))[1:]:
+        dma("shp%d" % j, row * (b - a), w2[0][:, C + a:C + b], T.shp[:, f:f + b - a], [], keys("s0", a, b))
     dma("thr", 128, T.thi[0:8, :], T.thr[:, :], [], ["thi"])
     dma("inc", row * C // 2, slot[4], T.inc[:, :], [], ["slot4"])
-    dma("exA", row * C // 2, T.w23[:, 0:C // 2], T.ex[:, 0:C // 2], [], ["ex3A"])
-    dma("exB", row * C // 2, T.w23[:, C // 2:C], T.ex[:, C // 2:C], [], ["ex3B"])
+    dma("exA", row * C // 2, w2[3][:, 0:C // 2], T.ex[:, 0:C // 2], [], ["ex3A"])
+    dma("exB", row * C // 2, w2[3][:, C // 2:C], T.ex[:, C // 2:C], [], ["ex3B"])
 
     op("G", "g", 1, lambda q: q.iota(T.pi[:, 0:1], [[0, 1]], 0, 1), [], ["pi"])
-    iota(T.row3[:, :, :], [[1, 128]], 0, 0, "row3")
     iota(T.row[:, :], [[1, 144]], -15, 0, "row")
+    clear(1)
+    iota(T.cst[:, 1:4], [[SL // 4, 3]], SL // 4, 0, "cst")
+    iota(T.big[:, 0:SL // 4], [[1, SL // 4]], 0, 0, "big0")
     iota(T.gi[0:8, :], [[1, 8], [0, 16]], 0, -1, "gi")
-    iota(T.fi[:, 0:32], [[16, 32]], C, 0, "fi")
-    iota(T.fi[:, 32:36], [[16, 4]], int(X0) + Z, 0, "fj")
+    iota(T.fi[:, 0:32], [[16, 32]], E + C, 0, "fi")
+    iota(T.fi[:, 32:36], [[16, 4]], Z, 0, "fj")
     iota(T.fi[:, 36:39], [[256, 3]], 256, 0, "fk")
-    iota(T.big[:, 0:SL // 4], [[1, SL // 4]], int(X0), 0, "big0")
-    iota(T.ki[:, :], [[-16, 4], [1, 64]], 0, 0, "ki")
+    iota(T.big[:, 3 * SL // 4:SL], [[1, SL // 4]], 3 * SL // 4, 0, "big3")
     V(136, lambda q: q.memset(T.sv[:, 0:17, :], 0.0), [], ["selv0"])
     V(280, lambda q: q.memset(T.sc[:, 0:70, :], 0.0), [], ["selc0"])
     for j, bits in enumerate((127, 15, 112)):
@@ -173,57 +195,66 @@ def build(T, topo, core, rank, prm):
     V(1, lambda q: q.memset(T.cst[:, 0:1], -TINY), [], ["tiny"])
     V(3, lambda q: q.tensor_copy(T.pf[:, 0:3], T.pj[:, 0:3]), ["pj0", "pj1", "pj2"], ["pf"])
     V(8, lambda q: q.memset(T.xf[:, :, 0:4], 0.0), [], ["xo%d" % t for t in range(NT)])
-    V(128, lambda q: q.tensor_scalar(T.id3[:, :, :], T.row3[:, :, :], own, None, A.is_equal), ["row3", "pf"], ["id3"])
+    V(128, lambda q: q.tensor_scalar(T.id3[:, :, :], T.row[:, 15:143], own, None, A.is_equal), ["row", "pf"], ["id3"])
     select(0)
     V(128, lambda q: q.tensor_scalar(eye[:, 0:128], T.row[:, 15:143], own, None, A.is_equal), ["row", "pf"], ["eye"])
     V(144, lambda q: q.tensor_scalar(T.ee[:, :], T.row[:, :], grp, None, A.is_equal), ["row", "pf"], ["ee"])
     S(128, lambda q: q.activation(neg, eye, AF.Copy, scale=-1.0), ["eye"], ["neg"])
     S(144, lambda q: q.activation(T.eh[:, :], T.ee[:, :], AF.Copy, scale=0.5), ["ee"], ["eh"])
-    for j in (1, 2, 3):
-        V(1, lambda q, j=j: q.memset(T.cst[:, j:j + 1], float(j * SL // 4)), [], ["cst%d" % j])
-        S(SL // 4, lambda q, j=j: q.activation(T.big[:, j * SL // 4:(j + 1) * SL // 4], T.big[:, 0:SL // 4], AF.Identity, bias=T.cst[:, j:j + 1]), ["big0", "cst%d" % j], ["big%d" % j])
     V(16, lambda q: q.tensor_scalar(T.m16[:, :], T.row[:, 15:31], low, None, A.is_equal), ["row", "pf"], ["m16"])
     V(16, lambda q: q.memset(T.p2[:, 32:48], 2.0), [], ["two"])
     V(16, lambda q: q.memset(T.p2[:, 48:64], 0.5), [], ["half"])
-    V(32, lambda q: q.memset(T.p2[:, 0:32], 0.0), [], ["p2a", "p2b"])
+    V(32, lambda q: q.memset(T.p2[:, 0:32], 0.0), [], ["p2z"])
     V(16, lambda q: q.memset(T.pm[:, 0:16], 0.0), [], ["pm0"])
+    for j, x in enumerate((-1024.0 - E, -0.5, 1.0)):
+        V(1, lambda q, j=j, x=x: q.memset(T.p2[:, M + j:M + j + 1], x), ["p2z"], ["p2c%d" % j])
+    V(M, lambda q: q.tensor_tensor_scan(T.p2[:, 0:M], T.p2[:, 32:32 + M], T.pm[:, 0:M], 0.25, A.mult, A.add), ["two", "pm0", "p2z"], ["p2a"])
+    V(M, lambda q: q.tensor_tensor_scan(T.p2[:, 16:16 + M], T.p2[:, 48:48 + M], T.pm[:, 0:M], 4.0 * SURE, A.mult, A.add), ["half", "pm0", "p2z"], ["p2b"])
+    V(4, lambda q: q.tensor_copy(T.ofs32[:, :], T.ofi[:, :]), ["ofi"], ["ofs32"])
+    for c in range(nc):
+        now[:] = [c, None]
+        first(c)
+    now[:] = [0, "k1"]
     for t in range(NT):
         (k, n, a, st), = runs([e[0] for e in plans[t][2]])
         V(3, lambda q, t=t, a=a, st=st: q.tensor_reduce(T.ind[:, t:t + 1], T.m16[:, a:a + 2 * st + 1:st], AxisListType.X, A.add), ["m16"], ["ind%d" % t])
-    V(M, lambda q: q.tensor_tensor_scan(T.p2[:, 0:M], T.p2[:, 32:32 + M], T.pm[:, 0:M], 0.25, A.mult, A.add), ["two", "pm0"], ["p2a"])
-    V(M, lambda q: q.tensor_tensor_scan(T.p2[:, 16:16 + M], T.p2[:, 48:48 + M], T.pm[:, 0:M], 4.0, A.mult, A.add), ["half", "pm0"], ["p2b"])
-    V(4, lambda q: q.tensor_copy(T.ofs32[:, :], T.ofi[:, :]), ["ofi"], ["ofs32"])
-    first(0)
     indk = ["ind%d" % t for t in range(NT)]
-    V(4, lambda q: q.tensor_scalar(T.ba[:, :], T.ind[:, :], 8.0, -7.5, A.mult, A.add), indk, ["ba"])
-    V(1, lambda q: q.memset(T.p2[:, M:M + 1], -1024.0), ["p2a"], ["p2c"])
-    V(1, lambda q: q.memset(T.p2[:, M + 1:M + 2], 0.5), ["p2a"], ["p2d"])
-    V(4, lambda q: q.tensor_scalar(T.bs[:, :], T.ind[:, :], 8.0, -8.5, A.mult, A.add), indk, ["bs"])
+    now[1] = "k2"
     for j in range(2):
         V(32, lambda q, j=j: q.tensor_tensor(T.pm[:, 16 * j:16 * j + 16], T.p2[:, 16 * j:16 * j + 16], T.m16[:, :], A.mult),
-          ["p2a", "p2b", "p2c", "p2d", "m16"], ["pm%d" % j])
-    V(6, lambda q: q.tensor_tensor(T.ob[:, 0:3], T.ofs32[:, 1:4], T.fi[:, 36:39], A.add), ["ofs32", "fk"], ["ob0"])
-    now[0] = -1
+          ["p2a", "p2b", "p2c0", "p2c1", "p2c2", "m16"], ["pm%d" % j])
+    V(4, lambda q: q.tensor_scalar(T.ba[:, :], T.ind[:, :], 8.0, -7.5, A.mult, A.add), indk, ["ba"])
+    V(4, lambda q: q.tensor_scalar(T.bs[:, :], T.ind[:, :], 8.0, -8.5, A.mult, A.add), indk, ["bs"])
+    now[1] = "k3"
     for j in range(2):
         V(16, lambda q, j=j: q.tensor_reduce(T.pc[:, j:j + 1], T.pm[:, 16 * j:16 * j + 16], AxisListType.X, A.add), ["pm%d" % j], ["pc%d" % j])
     V(128, lambda q: q.tensor_scalar(T.gm[0:8, :], T.gi[0:8, :], 0.0, None, A.is_equal), ["gi"], ["gm"])
+    now[1] = "k4"
+    V(32, lambda q: q.memset(T.ka[:, 0::2], FAR), [], ["ka0"])
+    V(32, lambda q: q.memset(T.ka[:, 1::2], -FAR), [], ["ka1"])
+    V(32, lambda q: q.memset(T.kb[:, 0::2], -FAR), [], ["kb0"])
+    V(32, lambda q: q.tensor_scalar(T.kb[:, 1::2], T.fi[:, 0:32], low, None, A.add), ["fi", "pf"], ["kb1"])
+    now[1] = "k5"
     V(144, lambda q: q.tensor_scalar(T.ew[:, :], T.ee[:, :], T.pc[:, 0:1], None, A.mult), ["ee", "pc0"], ["ew"])
-    for c in range(1, nc):
-        now[0] = c - 1
-        first(c, "x1")
-    now[0] = -1
-    V(4, lambda q: q.tensor_copy(T.thb[0:8, 0:4], T.thi[0:8, :]), ["thi"], ["thb"], "ub")
-    PE([4], lambda q: q.matmul(T.zp1[:, 0, 0:4], T.gm[0:8, :], T.thb[0:8, 0:4], True, True), ["gm", "thb"], ["zp1"], "sm")
-    V(200, lambda q: q.memset(T.w1[:, :, 0:Z + K], 0.0), [], ["spare%d" % t for t in range(5)], "xf")
-    V(36, lambda q: q.tensor_scalar(T.ff[:, :], T.fi[:, 0:36], low, None, A.add), ["fi", "fj", "pf"], ["ff"], "xf")
-    V(4, lambda q: q.tensor_copy(T.thf[:, :], T.zp1[:, 0, 0:4]), ["zp1"], ["thf"], "xf")
-    V(408, lambda q: q.memset(T.sv[:, 17:68, :], 0.0), [], ["selv1"], "sc")
-    V(840, lambda q: q.memset(T.sc[:, 70:280, :], 0.0), [], ["selc1"], "sc")
-    V(256, lambda q: q.tensor_scalar(T.kc[:, :], T.ki[:, :], low, None, A.is_equal), ["ki", "pf"], ["kc"], "mg")
+    V(E, lambda q: q.memset(T.w2[:, 0:E], 0), [], ["pad"])
+    now[1] = "k6"
+    V(200, lambda q: q.memset(T.w1[:, :, 0:Z + K], 0.0), [], ["spare%d" % t for t in range(5)])
+    V(6, lambda q: q.tensor_tensor(T.ob[:, 0:3], T.ofs32[:, 1:4], T.fi[:, 36:39], A.add), ["ofs32", "fk"], ["ob0"])
+    now[1] = "k7"
+    V(4, lambda q: q.tensor_scalar(T.ff[:, 32:36], T.fi[:, 32:36], low, None, A.add), ["fj", "pf"], ["ff"])
+    for a in range(4):
+        V(K, lambda q, a=a: q.tensor_scalar(T.kc[:, K * a:K * a + K], T.row[:, 15:15 + K], -16.0 * a, low, A.add, A.is_equal), ["row", "pf"], ["kc%d" % a], "k8")
+    V(4, lambda q: q.tensor_copy(T.thb[0:8, 0:4], T.thi[0:8, :]), ["thi"], ["thb"], "t1")
+    PE([4], lambda q: q.matmul(T.zp0[:, 0:4], T.gm[0:8, :], T.thb[0:8, 0:4], True, True), ["gm", "thb"], ["zp0"], "t2")
+    V(4, lambda q: q.tensor_scalar(T.thf[:, :], T.zp0[:, 0:4], -SURE, SURE, A.mult, A.add), ["zp0"], ["thf"], "t3")
+    V(4, lambda q: q.tensor_scalar(T.pq[:, :], T.thf[:, :], T.m16[:, M + 2:M + 3], T.pc[:, 1:2], A.mult, A.add), ["thf", "m16", "pc1"], ["pq"], "t4")
+    for j in (1, 2):
+        S(SL // 4, lambda q, j=j: q.activation(T.big[:, j * SL // 4:(j + 1) * SL // 4], T.big[:, 0:SL // 4], AF.Identity, bias=T.cst[:, j:j + 1]), ["big0", "cst"], ["big%d" % j], "b%d" % j)
+    now[1] = "s1"
+    select(1)
     for t in (1, 2, 3):
-        now[0] = prm["SEL"][t - 1]
-        select(t)
-        S(8, lambda q, t=t: q.activation(T.xf[:, nc * t:nc * t + nc, 0:4], T.xf[:, 0:nc, 0:4], AF.Identity, bias=T.ob[:, t - 1:t]), ["xo0", "ob0"], ["xo%d" % t])
+        S(8, lambda q, t=t: q.activation(T.xf[:, t, 0:4], T.xf[:, 0, 0:4], AF.Identity, bias=T.ob[:, t - 1:t]), ["xo0", "ob0"], ["xo%d" % t], "s2")
+    now[1] = None
 
     def again(a, b, at):
         op("G", "g", b - a, lambda q: q.affine_select(T.pw[:, at:at + b - a], T.pw[:, LO + a:LO + b], [[0, b - a]], A.is_ge, 0.0, 0, 0), ["pw"], ["pw%d" % at])
@@ -231,16 +262,16 @@ def build(T, topo, core, rank, prm):
 
     D, gp = 256, prm["GP"]
     wide = {0: ["pw"], 1: ["pw", "rep0", "rep3"]}
-    again(0, 512, LO + P)
+    again(0, 640, LO + P)
     send("in0", row * C // 2, 1, slot[0], slot[4], ["slot4"], ["slot0"])
-    again(512, 1024, LO + P + 512)
-    send("ex0A", row * C // 2, 1, T.w20[:, 0:C // 2], T.w23[:, 0:C // 2], ["ex3A"], ["ex0A"])
+    again(640, 1024, LO + P + 640)
+    send("ex0A", row * C // 2, 1, w2[0][:, 0:C // 2], w2[3][:, 0:C // 2], ["ex3A"], ["ex0A"])
     again(1024, 1536, LO + P + 1024)
-    send("ex0B", row * C // 2, 1, T.w20[:, C // 2:C], T.w23[:, C // 2:C], ["ex3B"], ["ex0B"])
+    send("ex0B", row * C // 2, 1, w2[0][:, C // 2:C], w2[3][:, C // 2:C], ["ex3B"], ["ex0B"])
     again(1536, gp, LO + P + 1536)
     send("in1", row * C // 2, 1, slot[1], slot[0], ["slot0"], ["slot1"])
-    send("ex1", row * C, 2, T.w21[:, 0:C], T.w23[:, 0:C], ["ex3A", "ex3B"], ["ex1A", "ex1B"])
     again(gp, P, LO + P + gp)
+    send("ex1", row * C, 2, w2[1][:, 0:C], w2[3][:, 0:C], ["ex3A", "ex3B"], ["ex1A", "ex1B"])
     dma("rep0", 128 * D * 2, T.pw[:, LO - D:LO], T.pic[:, P - D:P], [], ["rep0"])
     dma("rep3", 128 * D * 2, T.pw[:, LO + 2 * P:LO + 2 * P + D], T.pic[:, 0:D], [], ["rep3"])
     dma("rep1", 128 * (LO - D) * 2, T.pw[:, 0:LO - D], T.pic[:, P - LO:P - D], ["@ex1"], ["rep1"])
@@ -248,37 +279,39 @@ def build(T, topo, core, rank, prm):
     wide[2] = wide[3] = wide[1] + ["rep1", "rep2"]
 
     def lists(t, k, f0, f1):
-        H = f1 - f0
-
-        def fn(q, j, per, out):
-            sel, b = (T.sv, 17 * t + 1) if j == 0 else (T.sc, 35 * (2 * t + j - 1) + 3)
+        def fn(q, j, per, out, a, b):
+            sel, s0 = (T.sv, 17 * t + 1) if j == 0 else (T.sc, 35 * (2 * t + j - 1) + 3)
             for h in range(per):
-                ins = q.matmul(out, sel[:, b - h:b - h + 8 * per, :], T.xf[:, k, 4 - per + h:4 + H:per], h == 0, h == per - 1)
+                ins = q.matmul(out, sel[:, s0 - h:s0 - h + 8 * per, :], T.xf[:, t, a + h:b:per], h == 0, h == per - 1)
             return ins
-        for j, per, ps, c0, dst, bank, sk in ((0, 2, T.lv, 0, T.ov[:, f0 // 2:f1 // 2], "lv", selk[t][0] + selk[t][1]),
-                                              (1, 4, T.lc, 0, T.oc[:, f0 // 2:f0 // 2 + H // 4], "lc", selk[t][2]),
-                                              (2, 4, T.lv, 256, T.oc[:, f0 // 2 + H // 4:f1 // 2], "lv", selk[t][3])):
-            n, x = H // per, "vlr"[j]
-            PE([n + 1] * per, lambda q, j=j, per=per, out=ps[:, c0:c0 + n + 1]: fn(q, j, per, out), sk + ["xf%d" % k, "xo%d" % t], [bank], "l" + x, 4)
-            V(n, lambda q, dst=dst, src=ps[:, c0 + 1:c0 + n + 1], ofs=ps[:, c0:c0 + 1]: q.tensor_scalar(dst, src, ofs, None, A.add), [bank], keys("o" + x, f0, f1), ("ov", "ol", "Or")[j])
+        lead = int(f0 == 0)
+        for j, per, ps, c0, dst, bank, sk in ((0, 2, T.lv, 0, T.ov, "lv", selk[t][0] + selk[t][1]), (1, 4, T.lc, 0, T.ol, "lc", selk[t][2]),
+                                              (2, 4, T.lr, 0, T.oc, "lr", selk[t][3])):
+            g1 = f1 if j == 0 or lead or not prm["JOIN"] else F
+            if j and prm["JOIN"] and f1 == F:
+                continue
+            n, x = (g1 - f0) // per, "vlr"[j]
+            PE([n + lead] * per, lambda q, j=j, per=per, out=ps[:, c0 + 1 - lead:c0 + n + 1], g1=g1: fn(q, j, per, out, 4 + f0 - per * lead, 4 + g1),
+               sk + keys("xf%d_" % t, f0, g1) + ["xo%d" % t], [bank], "l" + x, 4)
+            V(n, lambda q, dst=dst[:, f0 // per:g1 // per], src=ps[:, c0 + 1:c0 + n + 1], ofs=ps[:, c0:c0 + 1]: q.tensor_scalar(dst, src, ofs, None, A.add),
+              [bank], keys("o" + x, f0, g1), ("ov", "ol", "Or")[j])
 
     def patch(t):
-        V(4, lambda q: q.tensor_scalar(T.tl[:, :], mi[t][:, K:K + 4], -X0, None, A.add), ["mi%d" % t], ["tl"], "tl")
+        V(4, lambda q: q.tensor_copy(T.tl[:, :], mi[t][:, K:K + 4]), ["mi%d" % t], ["tl"], "tl")
         V(K, lambda q: q.tensor_copy(T.w1[:, t, :].indirect(T.tl[:, :]), mi[t][:, 0:K]),
           ["tl", "mi%d" % t, "mh%d" % t], ["slot%d" % t, "spare%d" % t], "sca", "sca")
         if t == 3:
             V(K, lambda q: q.tensor_copy(T.w1[:, 4, :].indirect(T.tl[:, :]), mi[t][:, 0:K]), ["tl", "mi3", "mh3"], ["slot4", "spare4"], "sc4", "sca")
 
     def piece(t, f0, f1, a, b, j, bank, c0, x):
-        n, q4 = b - a, (f1 - f0) // 4
+        n = b - a
         win, wk = T.pw[:, LO - D * t:LO + D * t + (2 * P if t else P)], wide[t]
         left, right, pairs = plans[t]
         uk = keys("u", a, b)
         S(8 * n, lambda q: q.activation(T.u[:, 8 * a:8 * b], win.indirect(T.ov[:, a // 2:b // 2]), AF.Copy), wk + keys("ov", a, b), uk, "u" + x, "gat")
-        for out, name, l0, w, cmp in ((T.cl, "cl", 0, 0, A.is_gt), (T.cr, "cr", q4, RIGHT[t], A.is_lt)):
-            c1 = f0 // 2 + l0 + (a - f0) // 4
-            V(4 * n, lambda q, out=out, c1=c1, w=w, cmp=cmp: q.tensor_tensor(out[:, 4 * a:4 * b], win.indirect(T.oc[:, c1:c1 + n // 4]), T.u[:, 8 * a + w:8 * b:2], cmp),
-              wk + keys("o" + name[1], f0, f1) + uk, keys(name, a, b), name + x, "gat")
+        for out, name, lst, w, cmp in ((T.cl, "cl", T.ol, 0, A.is_gt), (T.cr, "cr", T.oc, RIGHT[t], A.is_lt)):
+            V(4 * n, lambda q, out=out, lst=lst, w=w, cmp=cmp: q.tensor_tensor(out[:, 4 * a:4 * b], win.indirect(lst[:, a // 4:b // 4]), T.u[:, 8 * a + w:8 * b:2], cmp),
+              wk + keys("o" + name[1], a, b) + uk, keys(name, a, b), name + x, "gat")
 
         def diffs(q):
             for e, (m, z, y) in enumerate(pairs):
@@ -300,55 +333,59 @@ def build(T, topo, core, rank, prm):
     def marks(t, a, b, bank, x):
         n, vk, cnt = b - a, "vp%d" % bank, vp[bank][:, 0:b - a]
         S(n, lambda q: q.activation(T.ab[:, a:b], cnt, AF.Abs, bias=T.ba[:, t:t + 1]), [vk, "ba"], keys("ab", a, b), "ab" + x)
-        S(n, lambda q: q.activation(T.ft[:, 0, a:b], cnt, AF.Sign, bias=T.bs[:, t:t + 1]), [vk, "bs"], keys("fb", a, b), "fb" + x)
-        V(n // 2, lambda q: q.tensor_scalar(T.ft[:, 1, a:b], T.ab[:, a:b], 4.0, T.pc[:, 1:2], A.is_ge, A.mult), keys("ab", a, b) + ["pc1"], keys("fe", a, b), "fe" + x)
+        S(n, lambda q: q.activation(T.ft[:, a:b, 1], cnt, AF.Sign, bias=T.bs[:, t:t + 1]), [vk, "bs"], keys("fb", a, b), "fb" + x)
+        V(n // 2, lambda q: q.tensor_scalar(T.ft[:, a:b, 0], T.ab[:, a:b], 4.0, T.pq[:, t:t + 1], A.is_ge, A.mult), keys("ab", a, b) + ["pq"], keys("fe", a, b), "fe" + x)
 
-    def tail(t, k, f0, f1, nys):
-        c = k % 2
-        n, na, a0, a1, zk = f1 - f0, (f1 - f0) // 16, f0 // 16, f1 // 16, "zp%d" % c
+    def tail(t, k, f0, f1, c):
+        n, na, a0, a1, zk = f1 - f0, (f1 - f0) // 16, f0 // 16, f1 // 16, ("zp0", "lr")[c]
 
         def sums(q):
             for b in range(16):
-                ins = q.matmul(zp[c][:, :, 0:na], T.ew[:, 15 - b:143 - b], T.ft[:, :, f0 + b:f1:16], b == 0, b == 15)
+                ins = q.matmul(zp[c][:, 0:2 * na], T.ew[:, 15 - b:143 - b], T.ft[:, f0 + b:f1:16, :], b == 0, b == 15)
             return ins
         PE([2 * na] * 16, sums, ["ew"] + keys("fb", f0, f1) + keys("fe", f0, f1), [zk], "sm")
-        ub, ta, tb = T.ub[:, a0:a1], T.ta[:, a0:a1], T.tb[:, a0:a1]
-        kub, kta, ktb, kia, kib, kup = (keys(x, f0, f1) for x in ("ub", "ta", "tb", "ia", "ib", "up"))
-        V(na, lambda q: q.tensor_scalar(ub, zp[c][:, 1, 0:na], T.thf[:, t:t + 1], SURE, A.is_ge, A.mult), [zk, "thf"], kub, "ub")
-        V(na, lambda q: q.tensor_tensor(ta, zp[c][:, 0, 0:na], ub, A.add), [zk] + kub, kta, "ta")
-        V(na, lambda q: q.tensor_scalar(T.ia[:, a0:a1], ta, -X0, None, A.add), kta, kia, "ia")
-        V(2 * na, lambda q: q.tensor_tensor(tb, ta, T.ff[:, a0:a1], A.min), kta + ["ff"], ktb, "tb")
-        V(na, lambda q: q.tensor_copy(T.ib[:, a0:a1], tb), ktb, kib, "ib")
-        S(n, lambda q: q.activation(T.up[:, f0:f1], T.w1[:, t, :].indirect(T.ia[:, a0:a1]), AF.Copy),
+        kta, ktb, kia, kup = (keys(x, f0, f1) for x in ("ta", "tb", "il", "up"))
+        V(2 * na, lambda q: q.tensor_tensor_scan(T.tt[:, 4 * a0:4 * a0 + 2 * na], T.ka[:, 0:2 * na], zp[c][:, 0:2 * na], 0.0, A.max, A.min), [zk, "ka0", "ka1"], kta, "ta")
+        V(2 * na, lambda q: q.tensor_tensor_scan(T.tt[:, 4 * a0 + 2 * na:4 * a1], T.kb[:, 2 * a0:2 * a1], zp[c][:, 0:2 * na], 0.0, A.min, A.max), [zk, "kb0", "kb1"], ktb, "tb")
+        V(2 * na, lambda q: q.tensor_copy(T.il[:, 2 * a0:2 * a1], T.tt[:, 4 * a0 + 1:4 * a1:2]), kta + ktb, kia, "il")
+        S(n, lambda q: q.activation(T.up[:, f0:f1], T.w1[:, t, :].indirect(T.il[:, 2 * a0:2 * a0 + na]), AF.Copy),
           ["slot%d" % t, "spare%d" % t] + kia, kup, "up", "gat")
-        new, nk = (T.xf[:, k + nc, 4:4 + n], ["xf%d" % (k + nc)]) if t < 3 else (T.xi[:, f0:f1], keys("xi", f0, f1))
-        V(n, lambda q: q.tensor_tensor(new, w2[t][:, 0:C + f1].indirect(T.ib[:, a0:a1]), T.up[:, f0:f1], A.add),
-          ["ex%dA" % t, "ex%dB" % t] + keys("s%d" % t, 0, f1) + kib + kup, nk, "xf", "gat")
+        new, nk = (T.xf[:, t + 1, 4 + f0:4 + f1], keys("xf%d_" % (t + 1), f0, f1)) if t < 3 else (T.xi[:, f0:f1], keys("xi", f0, f1))
+        V(n, lambda q: q.tensor_tensor(new, T.w2[:, WS * t:WS * t + E + C + f1].indirect(T.il[:, 2 * a0 + na:2 * a1]), T.up[:, f0:f1], A.add),
+          ["ex%dA" % t, "ex%dB" % t, "pad"] + keys("s%d" % (t - 1), F - E, F) + keys("s%d" % t, 0, f1) + kia + kup, nk, "xf", "gat")
         if t < 3 and prm["SC"] == "G":
             op("G", "g", n, lambda q: q.affine_select(w2[t + 1][:, C + f0:C + f1], new, [[0, n]], A.is_ge, 0.0, 0, 0), nk, keys("s%d" % (t + 1), f0, f1))
         elif t < 3:
             V(n, lambda q: q.tensor_copy(w2[t + 1][:, C + f0:C + f1], new), nk, keys("s%d" % (t + 1), f0, f1), "sc")
         else:
             V(n, lambda q: q.tensor_scalar(T.xj[:, f0:f1], T.xi[:, f0:f1], P - 1, None, A.bitwise_and), nk, keys("xj", f0, f1), "And")
-            V(n, lambda q: q.tensor_copy(T.yf[:, f0:f1], T.xj[:, f0:f1]), keys("xj", f0, f1), keys("yf", f0, f1), "yf")
-            dma("ys%d" % nys, row * n, T.ys[:, f0:f1], T.yf[:, f0:f1], keys("yf", f0, f1), [])
-        if f0 <= K * t < f1:
-            halve(t, kta + kia, kup)
+            if k < 4 * nc - 1:
+                op("G", "g", n, lambda q: q.affine_select(T.yf[:, f0:f1], T.xj[:, f0:f1], [[0, n]], A.is_ge, 0.0, 0, 0), keys("xj", f0, f1), keys("yf", f0, f1))
+            else:
+                V(n, lambda q: q.tensor_copy(T.yf[:, f0:f1], T.xj[:, f0:f1]), keys("xj", f0, f1), keys("yf", f0, f1), "yf")
+            for a, b, f in SEATS:
+                x, y = max(a, f0), min(b, f1)
+                if y > x:
+                    dma("ys%d" % count[1], row * (y - x), T.ys[:, f + x - a:f + y - a], T.yf[:, x:y], keys("yf", x, y), [])
+                    count[1] += 1
+        h = (t - 1) % NT
+        if f0 <= K * h < f1:
+            halve(t, h, T.il[:, a0 + 4 * h:a0 + 4 * h + 4], T.tt[:, 2 * a0 + 8 * h + 1:2 * a0 + 8 * h + 8:2], kta + kia, kup)
 
-    def halve(t, kt, kup):
+    def halve(t, h, lst, col, kt, kup):
         spare = T.ff[:, 32:36]
         mk, hk = ("mo%d" % t, "mg%d" % t) if t < 3 else ("mi4", "mh4")
         bk = ["big%d" % j for j in range(4)]
         for a in range(4):
-            out, src, mine = T.ne[:, K * a:K * a + K], T.big[:, :].indirect(T.ia[:, 4 * t:4 * t + 4]), T.ta[:, 4 * t + a:4 * t + a + 1]
+            out, src, mine = T.ne[:, K * a:K * a + K], T.big[:, :].indirect(lst), col[:, a:a + 1]
             if prm["NE"][a] == "V":
-                V(K, lambda q, out=out, src=src, mine=mine: q.tensor_scalar(out, src, mine, None, A.not_equal), bk + kt, ["ne%d" % a], "ne", "gat")
+                V(K, lambda q, out=out, src=src, mine=mine: q.tensor_scalar(out, src, mine, None, A.not_equal), bk + kt, ["ne%d" % a], "ne%d" % a, "gat")
             else:
-                S(K, lambda q, out=out, src=src, mine=mine: q.activation(out, src, AF.Abs, bias=mine, scale=-1.0), bk + kt, ["ne%d" % a], "ne", "gat")
-        V(128, lambda q: q.tensor_tensor_scan(T.kp[:, :], T.ne[:, :], T.kc[:, :], 0.0, A.min, A.max), ["ne0", "ne1", "ne2", "ne3", "kc"], ["kp"], "kp")
-        V(8, lambda q: q.tensor_tensor(T.ym[:, :], T.kp[:, K - 1::K], T.ta[:, 4 * t:4 * t + 4], A.mult), ["kp"] + kt, ["ym"], "ym")
+                S(K, lambda q, out=out, src=src, mine=mine: q.activation(out, src, AF.Abs, bias=mine, scale=-1.0), bk + kt, ["ne%d" % a], "ne%d" % a, "gat")
+        V(128, lambda q: q.tensor_tensor_scan(T.kp[:, :], T.ne[:, :], T.kc[:, :], 0.0, A.min, A.max), ["ne0", "ne1", "ne2", "ne3", "kc0", "kc1", "kc2", "kc3"], ["kp"], "kp")
+        V(8, lambda q: q.tensor_tensor(T.ym[:, :], T.kp[:, K - 1::K], col, A.mult), ["kp"] + kt, ["ym"], "ym")
         V(8, lambda q: q.tensor_tensor(mo[t][:, K:K + 4], T.ym[:, :], spare, A.max), ["ym", "ff"], [mk], "mo")
-        V(K, lambda q: q.tensor_scalar(mo[t][:, 0:K], T.up[:, K * t:K * t + K], 0.5, -0.25, A.mult, A.add), kup, [hk], "mg")
+        V(K, lambda q: q.tensor_scalar(mo[t][:, 0:K], T.up[:, K * h:K * h + K], 0.5, -0.25, A.mult, A.add), kup, [hk], "mg")
         if t < 3:
             send("m%d" % (t + 1), row * 68, 1, mi[t + 1][:, :], mo[t][:, :], [mk, hk], ["mi%d" % (t + 1), "mh%d" % (t + 1)])
         else:
@@ -366,18 +403,25 @@ def build(T, topo, core, rank, prm):
         if t in (1, 2):
             send("in%d" % (t + 1), row * C // 2, 1, slot[t + 1], slot[t], ["slot%d" % t], ["slot%d" % (t + 1)])
         if t == 1:
-            send("ex2", row * C, 3, T.w22[:, 0:C], T.w23[:, 0:C], ["ex3A", "ex3B"], ["ex2A", "ex2B"])
+            send("ex2", row * C, 3, w2[2][:, 0:C], w2[3][:, 0:C], ["ex3A", "ex3B"], ["ex2A", "ex2B"])
         for c, cut in enumerate(ch):
             now[0] = k = nc * t + c
-            f0, f1, last = cut[0], cut[-1], cut[-2] if prm["FS"] else -1
+            f0, f1, end = cut[0], cut[-1], k == NT * nc - 1
+            mid = prm["END"] if end else cut[1]
             lists(t, k, f0, f1)
-            for x, (a, b) in enumerate(zip(cut[:-1], cut[1:])):
-                bank = int(a == last) if prm["FS"] else k % 2
-                piece(t, f0, f1, a, b, count[0] % 2, bank, a if a == last else f0, str(x + 5 - len(cut)))
-                count[0] += 1
-                if b in (last, f1):
-                    marks(t, a if a == last else f0, b, bank, str(int(b == f1)))
-            tail(t, k, f0, f1, c)
+            piece(t, f0, f1, f0, mid, 0, (k + end) % 2, f0, "2")
+            if end:
+                early[0] = True
+                marks(t, f0, mid, (k + 1) % 2, "1")
+                tail(t, k, f0, mid, 1)
+                early[0] = False
+            g0 = mid if end else f0
+            piece(t, f0, f1, mid, f1, 1, k % 2, g0, "3")
+            marks(t, g0, f1, k % 2, "1")
+            tail(t, k, g0, f1, 0)
+        if t < 2:
+            clear(t + 2)
+            select(t + 2)
     return ops
 
 
@@ -409,50 +453,25 @@ def link(ops):
         o["deps"] = sorted(deps)
 
 
-def span(o):
-    n, cyc = o["n"], 0.87e-3
-    if o["kind"] == "mm":
-        return sum(max(64, x) for x in n) * o["w4"] * cyc / 2
-    if o["kind"] in ("gat", "sca"):
-        return 0.055 + n * cyc * (1.5 if o["kind"] == "gat" else 3.5)
-    if o["kind"] == "g":
-        return 0.15 + 2 * n * cyc
-    return {"dma": 0.1, "rem": 0.3}.get(o["kind"], max(64, n) * cyc)
+def schedule(ops, turn, nc):
+    place = {}
+    for part in turn:
+        for j, x in enumerate(turn[part].split()):
+            place[part[1:], x.strip("+-") if part[1:] == "round" else x] = (x.count("-") - x.count("+"), j)
 
-
-def schedule(ops, lag, wake=0.2, wait=0.05, fly=1.7, rate=450e3):
-    rank = [o["chunk"] + lag.get(o["tag"], 1) + i * 1e-6 for i, o in enumerate(ops)]
-    left, ready, users = [len(o["deps"]) for o in ops], [0.0] * len(ops), [[] for o in ops]
-    for i, o in enumerate(ops):
-        for j in o["deps"]:
-            users[j].append(i)
-    arr = {o["src"]: i for i, o in enumerate(ops) if o["kind"] == "arr"}
-    todo = {e: [i for i, o in enumerate(ops) if o["eng"] == e] for e in "VSPGY"}
-    pool = {e: [i for i in todo[e] if not left[i]] for e in "VSP"}
-    order, free, pipe = {e: [] for e in todo}, {e: 0.0 for e in todo}, 0.0
-
-    def done(i, t):
-        for j in users[i]:
-            ready[j] = max(ready[j], t if ops[i]["eng"] == "P" == ops[j]["eng"] else t + wake)
-            left[j] -= 1
-            if not left[j] and ops[j]["eng"] in pool:
-                pool[ops[j]["eng"]].append(j)
-    for step in range(sum(len(v) for v in todo.values())):
-        for e in "GY":
-            pool[e] = [i for i in todo[e][len(order[e]):len(order[e]) + 1] if not left[i]]
-        at, e = min((max(free[e], min(ready[i] for i in pool[e])), e) for e in pool if pool[e])
-        i = min((j for j in pool[e] if ready[j] <= at + wait), key=lambda j: rank[j])
-        pool[e].remove(i)
-        order[e].append(i)
-        free[e] = max(free[e], ready[i]) + span(ops[i])
-        if ops[i]["kind"] in ("dma", "rem"):
-            pipe = max(pipe, free[e] + 0.6 * fly) + ops[i]["n"] / rate
-            for j in (i, arr.get(i)):
-                if j is not None:
-                    done(j, pipe + 0.4 * fly)
-        else:
-            done(i, free[e])
-    return order
+    def at(i):
+        stage, tag = ops[i]["chunk"] // nc, ops[i]["tag"]
+        if not tag:
+            return (-2, 0, i)
+        x = tag + "ABC"[ops[i]["chunk"] % nc]
+        if ("start", x) in place:
+            return (-1, place["start", x][1], i)
+        last = ("end", x + "-" * (NT - 1 - stage))
+        if last in place and stage >= NT - 2:
+            return (NT, place[last][1], i)
+        return (stage + place["round", x][0], place["round", x][1], i)
+    mine = {e: [i for i, o in enumerate(ops) if o["eng"] == e] for e in "VSPGY"}
+    return {e: mine[e] if e in "GY" else sorted(mine[e], key=at) for e in mine}
 
 
 def rank_program(g, core, T, topo):
@@ -461,7 +480,7 @@ def rank_program(g, core, T, topo):
         return
     ops = build(T, topo, core, rank, PRM)
     link(ops)
-    order = schedule(ops, PRM["LAG"])
+    order = schedule(ops, PRM["TURN"], len(PRM["CH"]))
     queue = {"V": g.vector, "S": g.scalar, "P": g.tensor, "G": g, "Y": g.sync}
     needed = set()
     for o in ops:

from concourse.mybir import AluOpType, ActivationFunctionType, AxisListType

N, P, F, M, C, NT, K = 4, 4096, 512, 11, 2048, 4, 64
H = F // 2
LO = 768
PW = LO + 2 * P + LO
Z = 16
SL = Z + K + C
E = Z + K
SURE, FAR = 4096.0, 1e6
WS = C + F
TINY = 2.0 ** -108
BF, F32, I32, U16 = "bfloat16", "float32", "int32", "uint16"

ROWS = [([6, 7, 8, 9], [0, 5, 10, 15]), ([4, 5, 6, 7], [7, 8, 9, 10]), ([3, 4, 9, 10], [2, 5, 8, 11]), ([2, 6, 10, 3], [5, 7, 9, 11])]
RIGHT = [0, 1, 0, 0]

SCRATCH = {
    "pw": ("sbuf", [128, PW], BF), "u": ("sbuf", [128, F * 8], BF), "cl": ("sbuf", [128, F * 4], BF), "cr": ("sbuf", [128, F * 4], BF),
    "sg": ("sbuf", [128, 3, F], BF), "w1": ("sbuf", [128, 5, SL], BF),
    "w2": ("sbuf", [128, E + NT * WS], I32),
    "xi": ("sbuf", [128, F], I32), "xj": ("sbuf", [128, F], I32), "xf": ("sbuf", [128, NT, F + 4], F32), "yf": ("sbuf", [128, F], F32),
    "ov": ("sbuf", [128, F // 2], U16), "ol": ("sbuf", [128, F // 4], U16), "oc": ("sbuf", [128, F // 4], U16), "up": ("sbuf", [128, F], F32),
    "ab": ("sbuf", [128, F], BF), "ft": ("sbuf", [128, F, 2], BF),
    "ka": ("sbuf", [128, 64], F32), "kb": ("sbuf", [128, 64], F32), "tt": ("sbuf", [128, 128], F32), "il": ("sbuf", [128, 64], U16),
    "pq": ("sbuf", [128, 4], F32),
    "ofi": ("sbuf", [128, 4], I32), "ofs32": ("sbuf", [128, 4], F32), "ob": ("sbuf", [128, 4], F32), "oh": ("sbuf", [128, 4], F32),
    "thi": ("sbuf", [128, 4], I32), "thb": ("sbuf", [128, 8], BF), "thf": ("sbuf", [128, 4], F32),
    "row": ("sbuf", [128, 144], F32), "row3": ("sbuf", [128, 8, 16], F32), "big": ("sbuf", [128, SL], F32), "cst": ("sbuf", [128, 8], F32),
    "pi": ("sbuf", [128, 4], I32), "pj": ("sbuf", [128, 4], I32), "pf": ("sbuf", [128, 4], F32),
    "gi": ("sbuf", [128, 128], F32), "gm": ("sbuf", [128, 128], BF),
    "ee": ("sbuf", [128, 144], BF), "eh": ("sbuf", [128, 144], BF), "ew": ("sbuf", [128, 144], BF), "idm": ("sbuf", [128, 256], BF),
    "id3": ("sbuf", [128, 8, 16], F32), "sv": ("sbuf", [128, 4 * 17, 8], F32), "sc": ("sbuf", [128, 8 * 35, 4], F32),
    "m16": ("sbuf", [128, 16], F32), "p2": ("sbuf", [128, 64], F32), "pm": ("sbuf", [128, 32], F32), "pc": ("sbuf", [128, 4], F32),
    "ind": ("sbuf", [128, 4], F32), "ba": ("sbuf", [128, 4], F32), "bs": ("sbuf", [128, 4], F32),
    "fi": ("sbuf", [128, 40], F32), "ff": ("sbuf", [128, 36], F32),
    "ki": ("sbuf", [128, 256], F32), "kc": ("sbuf", [128, 256], BF),
    "y0": ("sbuf", [128, 4], F32), "yl": ("sbuf", [128, 4], U16), "ne": ("sbuf", [128, 256], BF),
    "kp": ("sbuf", [128, 256], BF), "ym": ("sbuf", [128, 4], F32), "tl": ("sbuf", [128, 4], U16),
    "mo0": ("sbuf", [128, 68], I32), "mo1": ("sbuf", [128, 68], I32), "mo2": ("sbuf", [128, 68], I32), "mo3": ("sbuf", [128, 68], I32),
    "mi1": ("sbuf", [128, 68], I32), "mi2": ("sbuf", [128, 68], I32), "mi3": ("sbuf", [128, 68], I32),
    "lv": ("psum", [128, 512], F32), "lc": ("psum", [128, 512], F32),
    "dp0": ("psum", [128, 4, 128], F32), "dp1": ("psum", [128, 4, 128], F32),
    "vp0": ("psum", [128, 512], F32), "vp1": ("psum", [128, 512], F32),
    "zp0": ("psum", [128, 512], F32), "lr": ("psum", [128, 512], F32),
}
BANKS = [n for n in SCRATCH if SCRATCH[n][0] == "psum"]
SEATS = [(0, 192, K), (192, 256, 0), (256, F, 256)]
DMAS = ["shp0", "shp1", "shp2", "ofs", "thr", "pic", "exA", "exB", "inc", "rep0", "rep3", "rep1", "rep2", "cp4", "yi", "ys0", "ys1", "ys2", "ys3", "ys4"]
SENDS = ["ex0A", "ex0B", "in0", "ex1", "ex2", "in1", "in2", "in3", "m1", "m2", "m3"]
SEMAPHORES = ["eV", "eS", "eP", "eG"] + ["d_" + n for n in DMAS] + ["l_" + n for n in SENDS] + ["r_" + n for n in SENDS]

TURN = {
    "Sstart": "s1A b1A b2A",
    "Vstart": "k8A x1A k1A x2A k2A x3A k3A k6A OVA k4A k7A k5A x1B x1C t1A x2B ORA x2C x3B OLA t3A x3C",
    "Pstart": "LVA LLA LRA t2A LVB",
    "Sround": "s2A u2A ne1B- ne0B- u3A upC- sg2A u2B sg3A u3B sg2B ab1A fb1A u2C sg3B u3C sg2C ab1B fb1B upA sg3C ne0A ne1A ab1C fb1C upB",
    "Vround": "mgA- kpA- fe1C- xfB- ymA- olA ne3B- mgB- moA- ne2B- OrA taC- tbC- cl2A kpB- ilC- OVB ovB cr2A ymB- cl3A moB- xfC- OrB cr3A ORB t4A "
              "olB OLB OVC cr2B cl2B ovC cr3B fe1A OLC ORC cl3B tlA olC OrC scaA cl2C tbA taA cr2C ilA cl3C fe1B cr3C xfA ne2A taB tbB ne3A ilB ovA+",
    "Pround": "lrA llA smC- lvB df2A LRB llB lrB LLB df3A vt2A LVC lvC df2B vt3A LLC llC lrC LRC df3B smA vt2B df2C vt3B df3C vt2C smB vt3C lvA+",
    "Send": "u2A u3A sg2A upC- u2B sg3A u3B sg2B ab1A fb1A u2C sg3B u3C ab1B fb1B sg2C sg3C upA ne1A AB1C ne0A FB1C ab1C fb1C upB UPC upC",
    "Vend": "fe1C- kpA- xfB- mgA- ymA- olA moA- OrA taC- tbC- cl2A ilC- ovB cr2A cl3A xfC- olB cr3A OrB cl2B tlA cr2B ovC cr3B fe1A cl3B olC scaA OrC "
            "sc4A cl2C taA tbA cr2C ilA cr3C fe1B ne3A cl3C ne2A xfA FE1C kpA AndA ymA taB tbB fe1C moA mgA ilB TLA TAC TBC SCAA ILC taC tbC xfB ilC "
            "AndB XFC xfC ANDC AndC YFC yfC",
    "Pend": "llA lrA smC- lvB df2A lrB llB df3A vt2A lvC df2B vt3A lrC llC df3B vt2B smA vt3B df2C df3C vt2C smB vt3C SMC smC",
}
PRM = dict(TURN=TURN, JOIN=False, GP=3072, END=448, NE="SSVV", SC="G", CH=[[0, 96, 192], [192, 272, 352], [352, 432, 512]])


def keys(name, a, b, step=16):
    return ["%s%d" % (name, j) for j in range(a // step, (b + step - 1) // step)]


def runs(lm):
    out, k = [], 0
    while k < len(lm):
        n, st = 1, 1
        if k + 1 < len(lm) and lm[k + 1] > lm[k]:
            st = lm[k + 1] - lm[k]
            while k + n < len(lm) and lm[k + n] - lm[k + n - 1] == st:
                n += 1
        out.append((k, n, lm[k], st))
        k += n
    return out


def plan(t):
    d, rows = 5 - t, ROWS[t]
    left, right = [q - d for q in rows[0]], [q + d for q in rows[RIGHT[t]]]
    place = {}
    for w in (1, 0):
        for k, q in enumerate(rows[w]):
            place[q] = 2 * k + w
    rest = [m for m in range(M) if m not in left and m not in rows[RIGHT[t]]]
    return left, right, [(m, place[m], place[m + d]) for m in rest]


def build(T, topo, core, rank, prm):
    A, AF = AluOpType, ActivationFunctionType
    ops, now, count, ch = [], [-9, None], [0, 0], prm["CH"]
    nc, early = len(ch), [False]
    mine = [(c, x) for c in range(nc) for x in "lv ov ll ol lr Or".split()] + [(4 * nc, "tl"), (4 * nc, "sca")]

    def op(eng, kind, n, fn, r, w, name=None, tag=None):
        tag = tag or now[1]
        if (now[0], tag) in mine or (tag and early[0]):
            tag = tag.upper()
        ops.append(dict(eng=eng, kind=kind, n=n, fn=fn, r=list(r), w=list(w), name=name, chunk=now[0], tag=tag))

    def V(n, fn, r, w, tag=None, kind="c"):
        op("V", kind, n, fn, r, w, None, tag)

    def S(n, fn, r, w, tag=None, kind="c"):
        op("S", kind, n, fn, r, w, None, tag)

    def PE(n, fn, r, w, tag=None, passes=1):
        op("P", "mm", n, fn, r, w, None, tag)
        ops[-1]["w4"] = passes

    def dma(name, nbytes, out, in_, r, w, eng="Y"):
        op(eng, "dma", nbytes, lambda q: q.dma_start(out, in_), r, w, name)

    def send(name, nbytes, hops, out, in_, r, w):
        dst = T.cores[(rank - hops) % N]
        rid, pid = topo.addr(dst)[0], topo.addr(dst)[1]
        mask = topo.mask(core, dst)
        op("G", "rem", nbytes, lambda q: q.remote_dma(out, in_, T.sem["r_" + name], T.sem["l_" + name], pid, rid, mask), r, [], name)
        ops[-1]["cnt"] = len(topo.engines(core, dst))
        op("R", "arr", nbytes, None, [], w, name)
        ops[-1]["cnt"] = len(topo.engines(T.cores[(rank + hops) % N], core))

    def iota(out, pattern, base, mult, key):
        n = pattern[0][1] * (pattern[1][1] if len(pattern) > 1 else 1)
        op("G", "g", n, lambda q: q.iota(out, pattern, base, mult, allow_small_or_imprecise_dtypes=True), [], [key])

    w2 = [T.w2[:, E + WS * t:E + WS * t + WS] for t in range(NT)]
    dp, vp, zp = [T.dp0, T.dp1], [T.vp0, T.vp1], [T.zp0, T.lr]
    mo, mi = [T.mo0, T.mo1, T.mo2, T.mo3], [None, T.mi1, T.mi2, T.mi3, T.mo3]
    slot = [T.w1[:, t, Z + K:SL] for t in range(5)]
    row = 128 * 4
    eye, neg = T.idm[:, 0:128], T.idm[:, 128:256]
    plans = [plan(t) for t in range(NT)]
    own, low, grp = T.pf[:, 0:1], T.pf[:, 1:2], T.pf[:, 2:3]
    selk = [[["sel%d_%d_%d" % (t, j, r[0]) for r in runs(lm)] for j, lm in enumerate(ROWS[t] + plans[t][0:2])] for t in range(NT)]

    def select(t):
        for j, lm in enumerate(ROWS[t] + plans[t][0:2]):
            for k, n, a, st in runs(lm):
                if j < 2:
                    out = T.sv[:, 17 * t + 1:17 * t + 17:2, 2 * k + j:2 * (k + n - 1) + j + 1:2]
                else:
                    out = T.sc[:, 35 * (2 * t + j - 2) + 3:35 * (2 * t + j - 1):4, k:k + n]
                src = T.id3[:, :, a:a + st * (n - 1) + 1:st]
                r, w = ["id3", ("selv%d" if j < 2 else "selc%d") % t], ["sel%d_%d_%d" % (t, j, k)]
                if t < 2:
                    S(8 * n, lambda q, out=out, src=src: q.activation(out, src, AF.Copy), r, w)
                else:
                    op("G", "g", 8 * n, lambda q, out=out, src=src, n=n: q.affine_select(out, src, [[0, 8 * n]], A.is_ge, 0.0, 0, 0), r, w)

    def clear(t):
        iota(T.sv[:, 17 * t:17 * t + 17, :], [[0, 136]], 0, 0, "selv%d" % t)
        iota(T.sc[:, 70 * t:70 * t + 70, :], [[0, 280]], 0, 0, "selc%d" % t)

    def first(c):
        f0, f1 = ch[c][0], ch[c][-1]
        n = f1 - f0
        V(n, lambda q: q.tensor_scalar(T.xi[:, f0:f1], w2[0][:, C + f0:C + f1], T.ofs32[:, 0:1], None, A.add), keys("s0", f0, f1) + ["ofs32"], keys("xi", f0, f1), "x1")
        V(n, lambda q: q.tensor_scalar(T.xj[:, f0:f1], T.xi[:, f0:f1], P - 1, None, A.bitwise_and), keys("xi", f0, f1), keys("xj", f0, f1), "x2")
        V(n, lambda q: q.tensor_copy(T.xf[:, 0, 4 + f0:4 + f1], T.xj[:, f0:f1]), keys("xj", f0, f1), keys("xf0_", f0, f1), "x3")

    dma("ofs", row * 4, T.ofi[:, :], T.ofs[:, :], [], ["ofi"])
    dma("shp0", row * 192, w2[0][:, C:C + 192], T.shp[:, K:K + 192], [], keys("s0", 0, 192), "S")
    dma("pic", 128 * P * 2, T.pw[:, LO:LO + P], T.pic[:, :], [], ["pw"])
    for j, (a, b, f) in list(enumerate(SEATS))[1:]:
        dma("shp%d" % j, row * (b - a), w2[0][:, C + a:C + b], T.shp[:, f:f + b - a], [], keys("s0", a, b))
    dma("thr", 128, T.thi[0:8, :], T.thr[:, :], [], ["thi"])
    dma("inc", row * C // 2, slot[4], T.inc[:, :], [], ["slot4"])
    dma("exA", row * C // 2, w2[3][:, 0:C // 2], T.ex[:, 0:C // 2], [], ["ex3A"])
    dma("exB", row * C // 2, w2[3][:, C // 2:C], T.ex[:, C // 2:C], [], ["ex3B"])

    op("G", "g", 1, lambda q: q.iota(T.pi[:, 0:1], [[0, 1]], 0, 1), [], ["pi"])
    iota(T.row[:, :], [[1, 144]], -15, 0, "row")
    clear(1)
    iota(T.cst[:, 1:4], [[SL // 4, 3]], SL // 4, 0, "cst")
    iota(T.big[:, 0:SL // 4], [[1, SL // 4]], 0, 0, "big0")
    iota(T.gi[0:8, :], [[1, 8], [0, 16]], 0, -1, "gi")
    iota(T.fi[:, 0:32], [[16, 32]], E + C, 0, "fi")
    iota(T.fi[:, 32:36], [[16, 4]], Z, 0, "fj")
    iota(T.fi[:, 36:39], [[256, 3]], 256, 0, "fk")
    iota(T.big[:, 3 * SL // 4:SL], [[1, SL // 4]], 3 * SL // 4, 0, "big3")
    V(136, lambda q: q.memset(T.sv[:, 0:17, :], 0.0), [], ["selv0"])
    V(280, lambda q: q.memset(T.sc[:, 0:70, :], 0.0), [], ["selc0"])
    for j, bits in enumerate((127, 15, 112)):
        V(1, lambda q, j=j, bits=bits: q.tensor_scalar(T.pj[:, j:j + 1], T.pi[:, 0:1], bits, None, A.bitwise_and), ["pi"], ["pj%d" % j])
    V(1, lambda q: q.memset(T.cst[:, 0:1], -TINY), [], ["tiny"])
    V(3, lambda q: q.tensor_copy(T.pf[:, 0:3], T.pj[:, 0:3]), ["pj0", "pj1", "pj2"], ["pf"])
    V(8, lambda q: q.memset(T.xf[:, :, 0:4], 0.0), [], ["xo%d" % t for t in range(NT)])
    V(128, lambda q: q.tensor_scalar(T.id3[:, :, :], T.row[:, 15:143], own, None, A.is_equal), ["row", "pf"], ["id3"])
    select(0)
    V(128, lambda q: q.tensor_scalar(eye[:, 0:128], T.row[:, 15:143], own, None, A.is_equal), ["row", "pf"], ["eye"])
    V(144, lambda q: q.tensor_scalar(T.ee[:, :], T.row[:, :], grp, None, A.is_equal), ["row", "pf"], ["ee"])
    S(128, lambda q: q.activation(neg, eye, AF.Copy, scale=-1.0), ["eye"], ["neg"])
    S(144, lambda q: q.activation(T.eh[:, :], T.ee[:, :], AF.Copy, scale=0.5), ["ee"], ["eh"])
    V(16, lambda q: q.tensor_scalar(T.m16[:, :], T.row[:, 15:31], low, None, A.is_equal), ["row", "pf"], ["m16"])
    V(16, lambda q: q.memset(T.p2[:, 32:48], 2.0), [], ["two"])
    V(16, lambda q: q.memset(T.p2[:, 48:64], 0.5), [], ["half"])
    V(32, lambda q: q.memset(T.p2[:, 0:32], 0.0), [], ["p2z"])
    V(16, lambda q: q.memset(T.pm[:, 0:16], 0.0), [], ["pm0"])
    for j, x in enumerate((-1024.0 - E, -0.5, 1.0)):
        V(1, lambda q, j=j, x=x: q.memset(T.p2[:, M + j:M + j + 1], x), ["p2z"], ["p2c%d" % j])
    V(M, lambda q: q.tensor_tensor_scan(T.p2[:, 0:M], T.p2[:, 32:32 + M], T.pm[:, 0:M], 0.25, A.mult, A.add), ["two", "pm0", "p2z"], ["p2a"])
    V(M, lambda q: q.tensor_tensor_scan(T.p2[:, 16:16 + M], T.p2[:, 48:48 + M], T.pm[:, 0:M], 4.0 * SURE, A.mult, A.add), ["half", "pm0", "p2z"], ["p2b"])
    V(4, lambda q: q.tensor_copy(T.ofs32[:, :], T.ofi[:, :]), ["ofi"], ["ofs32"])
    for c in range(nc):
        now[:] = [c, None]
        first(c)
    now[:] = [0, "k1"]
    for t in range(NT):
        (k, n, a, st), = runs([e[0] for e in plans[t][2]])
        V(3, lambda q, t=t, a=a, st=st: q.tensor_reduce(T.ind[:, t:t + 1], T.m16[:, a:a + 2 * st + 1:st], AxisListType.X, A.add), ["m16"], ["ind%d" % t])
    indk = ["ind%d" % t for t in range(NT)]
    now[1] = "k2"
    for j in range(2):
        V(32, lambda q, j=j: q.tensor_tensor(T.pm[:, 16 * j:16 * j + 16], T.p2[:, 16 * j:16 * j + 16], T.m16[:, :], A.mult),
          ["p2a", "p2b", "p2c0", "p2c1", "p2c2", "m16"], ["pm%d" % j])
    V(4, lambda q: q.tensor_scalar(T.ba[:, :], T.ind[:, :], 8.0, -7.5, A.mult, A.add), indk, ["ba"])
    V(4, lambda q: q.tensor_scalar(T.bs[:, :], T.ind[:, :], 8.0, -8.5, A.mult, A.add), indk, ["bs"])
    now[1] = "k3"
    for j in range(2):
        V(16, lambda q, j=j: q.tensor_reduce(T.pc[:, j:j + 1], T.pm[:, 16 * j:16 * j + 16], AxisListType.X, A.add), ["pm%d" % j], ["pc%d" % j])
    V(128, lambda q: q.tensor_scalar(T.gm[0:8, :], T.gi[0:8, :], 0.0, None, A.is_equal), ["gi"], ["gm"])
    now[1] = "k4"
    V(32, lambda q: q.memset(T.ka[:, 0::2], FAR), [], ["ka0"])
    V(32, lambda q: q.memset(T.ka[:, 1::2], -FAR), [], ["ka1"])
    V(32, lambda q: q.memset(T.kb[:, 0::2], -FAR), [], ["kb0"])
    V(32, lambda q: q.tensor_scalar(T.kb[:, 1::2], T.fi[:, 0:32], low, None, A.add), ["fi", "pf"], ["kb1"])
    now[1] = "k5"
    V(144, lambda q: q.tensor_scalar(T.ew[:, :], T.ee[:, :], T.pc[:, 0:1], None, A.mult), ["ee", "pc0"], ["ew"])
    V(E, lambda q: q.memset(T.w2[:, 0:E], 0), [], ["pad"])
    now[1] = "k6"
    V(200, lambda q: q.memset(T.w1[:, :, 0:Z + K], 0.0), [], ["spare%d" % t for t in range(5)])
    V(6, lambda q: q.tensor_tensor(T.ob[:, 0:3], T.ofs32[:, 1:4], T.fi[:, 36:39], A.add), ["ofs32", "fk"], ["ob0"])
    now[1] = "k7"
    V(4, lambda q: q.tensor_scalar(T.ff[:, 32:36], T.fi[:, 32:36], low, None, A.add), ["fj", "pf"], ["ff"])
    for a in range(4):
        V(K, lambda q, a=a: q.tensor_scalar(T.kc[:, K * a:K * a + K], T.row[:, 15:15 + K], -16.0 * a, low, A.add, A.is_equal), ["row", "pf"], ["kc%d" % a], "k8")
    V(4, lambda q: q.tensor_copy(T.thb[0:8, 0:4], T.thi[0:8, :]), ["thi"], ["thb"], "t1")
    PE([4], lambda q: q.matmul(T.zp0[:, 0:4], T.gm[0:8, :], T.thb[0:8, 0:4], True, True), ["gm", "thb"], ["zp0"], "t2")
    V(4, lambda q: q.tensor_scalar(T.thf[:, :], T.zp0[:, 0:4], -SURE, SURE, A.mult, A.add), ["zp0"], ["thf"], "t3")
    V(4, lambda q: q.tensor_scalar(T.pq[:, :], T.thf[:, :], T.m16[:, M + 2:M + 3], T.pc[:, 1:2], A.mult, A.add), ["thf", "m16", "pc1"], ["pq"], "t4")
    for j in (1, 2):
        S(SL // 4, lambda q, j=j: q.activation(T.big[:, j * SL // 4:(j + 1) * SL // 4], T.big[:, 0:SL // 4], AF.Identity, bias=T.cst[:, j:j + 1]), ["big0", "cst"], ["big%d" % j], "b%d" % j)
    now[1] = "s1"
    select(1)
    for t in (1, 2, 3):
        S(8, lambda q, t=t: q.activation(T.xf[:, t, 0:4], T.xf[:, 0, 0:4], AF.Identity, bias=T.ob[:, t - 1:t]), ["xo0", "ob0"], ["xo%d" % t], "s2")
    now[1] = None

    def again(a, b, at):
        op("G", "g", b - a, lambda q: q.affine_select(T.pw[:, at:at + b - a], T.pw[:, LO + a:LO + b], [[0, b - a]], A.is_ge, 0.0, 0, 0), ["pw"], ["pw%d" % at])
        wide[1].append("pw%d" % at)

    D, gp = 256, prm["GP"]
    wide = {0: ["pw"], 1: ["pw", "rep0", "rep3"]}
    again(0, 640, LO + P)
    send("in0", row * C // 2, 1, slot[0], slot[4], ["slot4"], ["slot0"])
    again(640, 1024, LO + P + 640)
    send("ex0A", row * C // 2, 1, w2[0][:, 0:C // 2], w2[3][:, 0:C // 2], ["ex3A"], ["ex0A"])
    again(1024, 1536, LO + P + 1024)
    send("ex0B", row * C // 2, 1, w2[0][:, C // 2:C], w2[3][:, C // 2:C], ["ex3B"], ["ex0B"])
    again(1536, gp, LO + P + 1536)
    send("in1", row * C // 2, 1, slot[1], slot[0], ["slot0"], ["slot1"])
    again(gp, P, LO + P + gp)
    send("ex1", row * C, 2, w2[1][:, 0:C], w2[3][:, 0:C], ["ex3A", "ex3B"], ["ex1A", "ex1B"])
    dma("rep0", 128 * D * 2, T.pw[:, LO - D:LO], T.pic[:, P - D:P], [], ["rep0"])
    dma("rep3", 128 * D * 2, T.pw[:, LO + 2 * P:LO + 2 * P + D], T.pic[:, 0:D], [], ["rep3"])
    dma("rep1", 128 * (LO - D) * 2, T.pw[:, 0:LO - D], T.pic[:, P - LO:P - D], ["@ex1"], ["rep1"])
    dma("rep2", 128 * (LO - D) * 2, T.pw[:, LO + 2 * P + D:PW], T.pic[:, D:LO], [], ["rep2"])
    wide[2] = wide[3] = wide[1] + ["rep1", "rep2"]

    def lists(t, k, f0, f1):
        def fn(q, j, per, out, a, b):
            sel, s0 = (T.sv, 17 * t + 1) if j == 0 else (T.sc, 35 * (2 * t + j - 1) + 3)
            for h in range(per):
                ins = q.matmul(out, sel[:, s0 - h:s0 - h + 8 * per, :], T.xf[:, t, a + h:b:per], h == 0, h == per - 1)
            return ins
        lead = int(f0 == 0)
        for j, per, ps, c0, dst, bank, sk in ((0, 2, T.lv, 0, T.ov, "lv", selk[t][0] + selk[t][1]), (1, 4, T.lc, 0, T.ol, "lc", selk[t][2]),
                                              (2, 4, T.lr, 0, T.oc, "lr", selk[t][3])):
            g1 = f1 if j == 0 or lead or not prm["JOIN"] else F
            if j and prm["JOIN"] and f1 == F:
                continue
            n, x = (g1 - f0) // per, "vlr"[j]
            PE([n + lead] * per, lambda q, j=j, per=per, out=ps[:, c0 + 1 - lead:c0 + n + 1], g1=g1: fn(q, j, per, out, 4 + f0 - per * lead, 4 + g1),
               sk + keys("xf%d_" % t, f0, g1) + ["xo%d" % t], [bank], "l" + x, 4)
            V(n, lambda q, dst=dst[:, f0 // per:g1 // per], src=ps[:, c0 + 1:c0 + n + 1], ofs=ps[:, c0:c0 + 1]: q.tensor_scalar(dst, src, ofs, None, A.add),
              [bank], keys("o" + x, f0, g1), ("ov", "ol", "Or")[j])

    def patch(t):
        V(4, lambda q: q.tensor_copy(T.tl[:, :], mi[t][:, K:K + 4]), ["mi%d" % t], ["tl"], "tl")
        V(K, lambda q: q.tensor_copy(T.w1[:, t, :].indirect(T.tl[:, :]), mi[t][:, 0:K]),
          ["tl", "mi%d" % t, "mh%d" % t], ["slot%d" % t, "spare%d" % t], "sca", "sca")
        if t == 3:
            V(K, lambda q: q.tensor_copy(T.w1[:, 4, :].indirect(T.tl[:, :]), mi[t][:, 0:K]), ["tl", "mi3", "mh3"], ["slot4", "spare4"], "sc4", "sca")

    def piece(t, f0, f1, a, b, j, bank, c0, x):
        n = b - a
        win, wk = T.pw[:, LO - D * t:LO + D * t + (2 * P if t else P)], wide[t]
        left, right, pairs = plans[t]
        uk = keys("u", a, b)
        S(8 * n, lambda q: q.activation(T.u[:, 8 * a:8 * b], win.indirect(T.ov[:, a // 2:b // 2]), AF.Copy), wk + keys("ov", a, b), uk, "u" + x, "gat")
        for out, name, lst, w, cmp in ((T.cl, "cl", T.ol, 0, A.is_gt), (T.cr, "cr", T.oc, RIGHT[t], A.is_lt)):
            V(4 * n, lambda q, out=out, lst=lst, w=w, cmp=cmp: q.tensor_tensor(out[:, 4 * a:4 * b], win.indirect(lst[:, a // 4:b // 4]), T.u[:, 8 * a + w:8 * b:2], cmp),
              wk + keys("o" + name[1], a, b) + uk, keys(name, a, b), name + x, "gat")

        def diffs(q):
            for e, (m, z, y) in enumerate(pairs):
                q.matmul(dp[j][:, e, 0:n], eye, T.u[:, 8 * a + z:8 * b:8], True, False)
                ins = q.matmul(dp[j][:, e, 0:n], neg, T.u[:, 8 * a + y:8 * b:8], False, True)
            return ins
        PE([n] * 6, diffs, ["eye", "neg"] + uk, ["dp%d" % j], "df" + x)
        S(3 * n, lambda q: q.activation(T.sg[:, :, a:b], dp[j][:, 0:3, 0:n], AF.Sign, bias=T.cst[:, 0:1]), ["dp%d" % j, "tiny"], keys("sg", a, b), "sg" + x)
        terms = [(T.eh, m, T.sg[:, e, a:b]) for e, (m, z, y) in enumerate(pairs)]
        terms += [(T.ee, m, T.cl[:, 4 * a + k:4 * b:4]) for k, m in enumerate(left)]
        terms += [(T.ee, m, T.cr[:, 4 * a + k:4 * b:4]) for k, m in enumerate(ROWS[t][RIGHT[t]])]

        def votes(q):
            for i, (wt, m, rhs) in enumerate(terms):
                ins = q.matmul(vp[bank][:, a - c0:b - c0], wt[:, 15 - m:143 - m], rhs, i == 0, i == M - 1)
            return ins
        PE([n] * M, votes, ["ee", "eh"] + keys("sg", a, b) + keys("cl", a, b) + keys("cr", a, b), ["vp%d" % bank], "vt" + x)

    def marks(t, a, b, bank, x):
        n, vk, cnt = b - a, "vp%d" % bank, vp[bank][:, 0:b - a]
        S(n, lambda q: q.activation(T.ab[:, a:b], cnt, AF.Abs, bias=T.ba[:, t:t + 1]), [vk, "ba"], keys("ab", a, b), "ab" + x)
        S(n, lambda q: q.activation(T.ft[:, a:b, 1], cnt, AF.Sign, bias=T.bs[:, t:t + 1]), [vk, "bs"], keys("fb", a, b), "fb" + x)
        V(n // 2, lambda q: q.tensor_scalar(T.ft[:, a:b, 0], T.ab[:, a:b], 4.0, T.pq[:, t:t + 1], A.is_ge, A.mult), keys("ab", a, b) + ["pq"], keys("fe", a, b), "fe" + x)

    def tail(t, k, f0, f1, c):
        n, na, a0, a1, zk = f1 - f0, (f1 - f0) // 16, f0 // 16, f1 // 16, ("zp0", "lr")[c]

        def sums(q):
            for b in range(16):
                ins = q.matmul(zp[c][:, 0:2 * na], T.ew[:, 15 - b:143 - b], T.ft[:, f0 + b:f1:16, :], b == 0, b == 15)
            return ins
        PE([2 * na] * 16, sums, ["ew"] + keys("fb", f0, f1) + keys("fe", f0, f1), [zk], "sm")
        kta, ktb, kia, kup = (keys(x, f0, f1) for x in ("ta", "tb", "il", "up"))
        V(2 * na, lambda q: q.tensor_tensor_scan(T.tt[:, 4 * a0:4 * a0 + 2 * na], T.ka[:, 0:2 * na], zp[c][:, 0:2 * na], 0.0, A.max, A.min), [zk, "ka0", "ka1"], kta, "ta")
        V(2 * na, lambda q: q.tensor_tensor_scan(T.tt[:, 4 * a0 + 2 * na:4 * a1], T.kb[:, 2 * a0:2 * a1], zp[c][:, 0:2 * na], 0.0, A.min, A.max), [zk, "kb0", "kb1"], ktb, "tb")
        V(2 * na, lambda q: q.tensor_copy(T.il[:, 2 * a0:2 * a1], T.tt[:, 4 * a0 + 1:4 * a1:2]), kta + ktb, kia, "il")
        S(n, lambda q: q.activation(T.up[:, f0:f1], T.w1[:, t, :].indirect(T.il[:, 2 * a0:2 * a0 + na]), AF.Copy),
          ["slot%d" % t, "spare%d" % t] + kia, kup, "up", "gat")
        new, nk = (T.xf[:, t + 1, 4 + f0:4 + f1], keys("xf%d_" % (t + 1), f0, f1)) if t < 3 else (T.xi[:, f0:f1], keys("xi", f0, f1))
        V(n, lambda q: q.tensor_tensor(new, T.w2[:, WS * t:WS * t + E + C + f1].indirect(T.il[:, 2 * a0 + na:2 * a1]), T.up[:, f0:f1], A.add),
          ["ex%dA" % t, "ex%dB" % t, "pad"] + keys("s%d" % (t - 1), F - E, F) + keys("s%d" % t, 0, f1) + kia + kup, nk, "xf", "gat")
        if t < 3 and prm["SC"] == "G":
            op("G", "g", n, lambda q: q.affine_select(w2[t + 1][:, C + f0:C + f1], new, [[0, n]], A.is_ge, 0.0, 0, 0), nk, keys("s%d" % (t + 1), f0, f1))
        elif t < 3:
            V(n, lambda q: q.tensor_copy(w2[t + 1][:, C + f0:C + f1], new), nk, keys("s%d" % (t + 1), f0, f1), "sc")
        else:
            V(n, lambda q: q.tensor_scalar(T.xj[:, f0:f1], T.xi[:, f0:f1], P - 1, None, A.bitwise_and), nk, keys("xj", f0, f1), "And")
            if k < 4 * nc - 1:
                op("G", "g", n, lambda q: q.affine_select(T.yf[:, f0:f1], T.xj[:, f0:f1], [[0, n]], A.is_ge, 0.0, 0, 0), keys("xj", f0, f1), keys("yf", f0, f1))
            else:
                V(n, lambda q: q.tensor_copy(T.yf[:, f0:f1], T.xj[:, f0:f1]), keys("xj", f0, f1), keys("yf", f0, f1), "yf")
            for a, b, f in SEATS:
                x, y = max(a, f0), min(b, f1)
                if y > x:
                    dma("ys%d" % count[1], row * (y - x), T.ys[:, f + x - a:f + y - a], T.yf[:, x:y], keys("yf", x, y), [])
                    count[1] += 1
        h = (t - 1) % NT
        if f0 <= K * h < f1:
            halve(t, h, T.il[:, a0 + 4 * h:a0 + 4 * h + 4], T.tt[:, 2 * a0 + 8 * h + 1:2 * a0 + 8 * h + 8:2], kta + kia, kup)

    def halve(t, h, lst, col, kt, kup):
        spare = T.ff[:, 32:36]
        mk, hk = ("mo%d" % t, "mg%d" % t) if t < 3 else ("mi4", "mh4")
        bk = ["big%d" % j for j in range(4)]
        for a in range(4):
            out, src, mine = T.ne[:, K * a:K * a + K], T.big[:, :].indirect(lst), col[:, a:a + 1]
            if prm["NE"][a] == "V":
                V(K, lambda q, out=out, src=src, mine=mine: q.tensor_scalar(out, src, mine, None, A.not_equal), bk + kt, ["ne%d" % a], "ne%d" % a, "gat")
            else:
                S(K, lambda q, out=out, src=src, mine=mine: q.activation(out, src, AF.Abs, bias=mine, scale=-1.0), bk + kt, ["ne%d" % a], "ne%d" % a, "gat")
        V(128, lambda q: q.tensor_tensor_scan(T.kp[:, :], T.ne[:, :], T.kc[:, :], 0.0, A.min, A.max), ["ne0", "ne1", "ne2", "ne3", "kc0", "kc1", "kc2", "kc3"], ["kp"], "kp")
        V(8, lambda q: q.tensor_tensor(T.ym[:, :], T.kp[:, K - 1::K], col, A.mult), ["kp"] + kt, ["ym"], "ym")
        V(8, lambda q: q.tensor_tensor(mo[t][:, K:K + 4], T.ym[:, :], spare, A.max), ["ym", "ff"], [mk], "mo")
        V(K, lambda q: q.tensor_scalar(mo[t][:, 0:K], T.up[:, K * h:K * h + K], 0.5, -0.25, A.mult, A.add), kup, [hk], "mg")
        if t < 3:
            send("m%d" % (t + 1), row * 68, 1, mi[t + 1][:, :], mo[t][:, :], [mk, hk], ["mi%d" % (t + 1), "mh%d" % (t + 1)])
        else:
            k, now[0] = now[0], 4 * nc
            patch(4)
            now[0] = k
            dma("yi", row * C // 2, T.yi[:, :], slot[4], ["slot4"], [])

    for t in range(NT):
        now[0] = nc * t
        if t == 3:
            dma("cp4", row * C // 2, slot[4], slot[3], ["slot3"], ["slot4"])
        if t > 0:
            patch(t)
        if t in (1, 2):
            send("in%d" % (t + 1), row * C // 2, 1, slot[t + 1], slot[t], ["slot%d" % t], ["slot%d" % (t + 1)])
        if t == 1:
            send("ex2", row * C, 3, w2[2][:, 0:C], w2[3][:, 0:C], ["ex3A", "ex3B"], ["ex2A", "ex2B"])
        for c, cut in enumerate(ch):
            now[0] = k = nc * t + c
            f0, f1, end = cut[0], cut[-1], k == NT * nc - 1
            mid = prm["END"] if end else cut[1]
            lists(t, k, f0, f1)
            piece(t, f0, f1, f0, mid, 0, (k + end) % 2, f0, "2")
            if end:
                early[0] = True
                marks(t, f0, mid, (k + 1) % 2, "1")
                tail(t, k, f0, mid, 1)
                early[0] = False
            g0 = mid if end else f0
            piece(t, f0, f1, mid, f1, 1, k % 2, g0, "3")
            marks(t, g0, f1, k % 2, "1")
            tail(t, k, g0, f1, 0)
        if t < 2:
            clear(t + 2)
            select(t + 2)
    return ops


def link(ops):
    last, readers = {}, {}
    sends = {o["name"]: i for i, o in enumerate(ops) if o["kind"] == "rem"}
    for i, o in enumerate(ops):
        deps = set()
        if o["kind"] == "arr":
            o["src"] = sends[o["name"]]
        for key in o["r"]:
            if key[0] == "@":
                deps.add(sends[key[1:]])
            elif key in last:
                deps.add(last[key])
            if key in BANKS:
                deps.update(j for j in readers.get(key, []) if ops[j]["eng"] != o["eng"])
        if o["kind"] != "arr":
            for key in o["w"]:
                if key in last:
                    deps.add(last[key])
                deps.update(readers.get(key, []))
        for key in o["r"]:
            readers.setdefault(key, []).append(i)
        for key in o["w"]:
            last[key] = i
            readers[key] = []
        deps.discard(i)
        o["deps"] = sorted(deps)


def schedule(ops, turn, nc):
    place = {}
    for part in turn:
        for j, x in enumerate(turn[part].split()):
            place[part[1:], x.strip("+-") if part[1:] == "round" else x] = (x.count("-") - x.count("+"), j)

    def at(i):
        stage, tag = ops[i]["chunk"] // nc, ops[i]["tag"]
        if not tag:
            return (-2, 0, i)
        x = tag + "ABC"[ops[i]["chunk"] % nc]
        if ("start", x) in place:
            return (-1, place["start", x][1], i)
        last = ("end", x + "-" * (NT - 1 - stage))
        if last in place and stage >= NT - 2:
            return (NT, place[last][1], i)
        return (stage + place["round", x][0], place["round", x][1], i)
    mine = {e: [i for i, o in enumerate(ops) if o["eng"] == e] for e in "VSPGY"}
    return {e: mine[e] if e in "GY" else sorted(mine[e], key=at) for e in mine}


def rank_program(g, core, T, topo):
    rank = T.rank_of(core)
    if rank is None:
        return
    ops = build(T, topo, core, rank, PRM)
    link(ops)
    order = schedule(ops, PRM["TURN"], len(PRM["CH"]))
    queue = {"V": g.vector, "S": g.scalar, "P": g.tensor, "G": g, "Y": g.sync}
    needed = set()
    for o in ops:
        for j in o["deps"]:
            if not (o["eng"] == "P" and ops[j]["eng"] == "P"):
                needed.add(j)
    mark = {}
    for e in "VSPG":
        cnt = 0
        for i in order[e]:
            if ops[i]["kind"] not in ("rem", "dma") and i in needed:
                cnt += 1
                mark[i] = ("e" + e, cnt)
    for i, o in enumerate(ops):
        if o["kind"] == "dma":
            mark[i] = ("d_" + o["name"], 16)
        elif o["kind"] == "rem":
            mark[i] = ("l_" + o["name"], o["cnt"])
        elif o["kind"] == "arr":
            mark[i] = ("r_" + o["name"], o["cnt"])
    top = {}
    for e in "SGVPY":
        q, seen = queue[e], {}
        for i in order[e]:
            o = ops[i]
            want = {}
            for j in o["deps"]:
                if e == "P" and ops[j]["eng"] == "P":
                    continue
                s, v = mark[j]
                want[s] = max(want.get(s, 0), v)
            for s in sorted(want):
                if want[s] > seen.get(s, 0):
                    q.wait_ge(T.sem[s], want[s])
                    seen[s] = want[s]
                    top[s] = max(top.get(s, 0), want[s])
            ins = o["fn"](q)
            if o["kind"] == "dma":
                ins.then_inc(T.sem[mark[i][0]], 16)
            elif o["kind"] != "rem" and i in mark:
                ins.then_inc(T.sem[mark[i][0]], 1)
    end = {}
    for s, v in mark.values():
        end[s] = max(end.get(s, 0), v)
    for s in sorted(end):
        if end[s] > top.get(s, 0):
            g.sync.wait_ge(T.sem[s], end[s])
